import numpy as np, ml_dtypes
CORES = [66,74,82,90,194,202,210,218]
N = 8
import mx_ref
BF = ml_dtypes.bfloat16
def gentries(a):
    return np.ascontiguousarray(a.reshape(8, 16, -1).transpose(0, 2, 1)).reshape(8, -1)
def gtable(e):
    e = np.asarray(e); return np.ascontiguousarray(e.reshape(8, -1, 16).transpose(0, 2, 1)).reshape(128, -1).astype(np.int32)
def gcols(t, e):
    v = np.concatenate([t.reshape(8, 16, -1, 4), np.zeros((8, 16, 1, 4), BF)], axis=2)
    return np.ascontiguousarray(np.stack([v[g][:, e[g]] for g in range(8)])).reshape(128, -1)
def tile(rs):
    return np.stack(rs, axis=2).reshape(128, -1).astype(BF)
def pick(q, e):
    c = np.concatenate([q[0].reshape(128, -1, 4), np.zeros((128, 1, 4), np.uint8)], axis=1); s = np.concatenate([q[1], np.ones((16, 1), np.uint8)], axis=1)
    return (np.ascontiguousarray(c[:, e].reshape(128, -1)), np.ascontiguousarray(s[:, e]))
def join(*qs):
    return (np.concatenate([q[0] for q in qs], axis=1), np.concatenate([q[1] for q in qs], axis=1))
def put(q, e, v):
    c, s = q[0].reshape(128, -1, 4).copy(), q[1].copy(); c[:, e] = v[0].reshape(128, -1, 4); s[:, e] = v[1]
    return (c.reshape(128, -1), s)
def pk(c, s):
    return (np.ascontiguousarray(c), mx_ref.live(s))
def emit(q):
    return q[0], q[1]
def packed(v, rng):
    q = [mx_ref.quantize(np.ascontiguousarray(v[r])) for r in range(N)]
    return np.stack([a for a, b in q]), np.stack([mx_ref.plane(b, rng) for a, b in q])
def values_of_codes():
    e, c = np.zeros((128, 128, 4), np.float32), np.zeros((128, 2, 4), np.uint8)
    e[np.arange(128), np.arange(128), 0] = 1
    c[:127, :, 0] = np.arange(256).reshape(2, 128).T[:127]
    return mx_ref.matmul(mx_ref.quantize(e.reshape(128, 512).astype(BF)), (c.reshape(128, 8), np.full((16, 2), 127, np.uint8))).T.reshape(-1).astype(np.float64)
CODE_VALUE, SCALE_VALUE = values_of_codes(), 2.0 ** (np.arange(256) - 127.0)
def decode(q):
    return (CODE_VALUE[q[0]].reshape(16, 8, -1, 4) * SCALE_VALUE[q[1]][:, None, :, None] + 0.0).reshape(128, -1).astype(np.float32)
def f(rng, *shape):
    return mx_ref.flush((rng.standard_normal(shape, dtype=np.float32) * np.exp2(rng.integers(-2, 3, shape[:-1] + (1,)))).astype(BF))
def wide(rng, *shape, cols=0):
    v = rng.standard_normal(shape, dtype=np.float32) * np.exp2(rng.integers(-12, 13, shape)).astype(np.float32)
    if cols: v *= np.repeat(np.exp2(rng.integers(-cols, cols + 1, shape[:-2] + (1, shape[-1] // 4))) * (rng.random(shape[:-2] + (1, shape[-1] // 4)) > 0.0625), 4, axis=-1).astype(np.float32)
    return mx_ref.flush(v.astype(BF))
C, F = 320, 240
MASK = [4, 1, 2]
def numbers_of(rng):
    return {"x": np.array(f(rng, N, 128, 4 * C)), "u": np.array(f(rng, N, 128, 512)), "v": np.array(f(rng, N, 128, 512))}
def stored(k, n):
    return {"dl": np.stack([gtable(k[r]) for r in range(N)]), "nl": np.stack([gtable(n[r]) for r in range(N)])}
def lists(rng):
    e = np.tile(np.arange(C), (N, 8, 1))
    k, e = rng.permuted(e, axis=2), rng.permuted(e, axis=2)
    n = np.empty_like(e)
    np.put_along_axis(n, e, e.reshape(N, 8, -1, 2)[..., ::-1].reshape(N, 8, C), axis=2)
    return k, n
def layers(rng, still=[]):
    w = np.array(f(rng, N, 128, 2048)).reshape(N, 8, 16, 4, 8, 16, 4)
    for i in still:
        w[:, :, i] = 0
        w[:, :, :, :, :, i] = 0
    return w
def weights(rng, w):
    c, s = packed(np.ascontiguousarray(w).reshape(N, 128, 2048), rng)
    return {"wc": c, "ws": s}
def setup_inputs(rng):
    return {**numbers_of(rng), **stored(*lists(rng)), **weights(rng, layers(rng))}
def setup_inputs_ties(rng):
    d = numbers_of(rng)
    k, n = lists(rng)
    o, h = rng.permutation(N), rng.permutation(8)
    i = np.arange(N)
    e = (i ^ (i >> 1) ^ (i >> 2)) % 2
    s = rng.integers(0, 4, (N, 8, C))
    s[o[1]] += 1
    s[:, h[:3]] = 1
    for g in h[:2]:
        for r in np.flatnonzero(e):
            k[r, g] = n[r, g]
            s[r, g] = np.where(np.arange(C) < n[r, g], 2, 0)
    c = np.ones((N, 8), np.float32)
    c[o[0]] = 0
    c[o[1]] = -1
    c[:, h[:3]] = 1
    x = d["x"].reshape(N, 8, 16, C, 4)
    x[:, :, 0] = 0
    x[:, :, 0, :, 0] = s.astype(np.float32).astype(BF)
    a = np.exp2(rng.integers(-3, 4, (1, 8, 1)).astype(np.float32))
    x[:, :, 8:] = 0
    x[:, :, 8, :, 0] = (-1.125 * a).astype(BF)
    x[:, :, 10, :, 0] = (-0.0703125 * a).astype(BF)
    u = d["u"].reshape(N, 128, 128, 4)
    u[:, :, ::16] = 0
    w = layers(rng, [0])
    w[:, :, :, :, :, 8:] = 0
    for g in range(8):
        u[:, 16 * g, 16 * g, 0] = c[:, g].astype(BF)
        w[:, g, 8, 0, g, 8, 0] = -28.0
        for b in range(4): w[:, g, 10, b, g, 9, 0] = -2.0 ** (b - 5)
    return {"x": x.reshape(N, 128, 4 * C), "u": u.reshape(N, 128, 512), "v": d["v"], **stored(k, n), **weights(rng, w)}
def setup_inputs_near(rng):
    d = numbers_of(rng)
    k, n = lists(rng)
    x = d["x"].astype(np.float32).reshape(N, 8, 16, C, 4)
    x[:, :, 0] = 0
    x[:, :, 8:] = 0
    u = d["u"].reshape(N, 128, 128, 4)
    u[:, :, ::16] = 0
    w = layers(rng, [0, 8, 9, 10, 11, 12, 13, 14, 15])
    at = [0, C - 1, int(rng.integers(C)), int(rng.integers(C))]
    for i, g in enumerate(rng.permutation(8)):
        h, c = 16 * g, 1.0 if i < 2 else 2.0 ** -30
        s = rng.integers(0, 16, (N, C))
        digits = ((s[:, :, None] >> np.arange(4)) & 1) * np.exp2(np.arange(4) - 23.0)
        u[:, h, h, 0] = c
        if i < 4:
            x[:, g, 0, :, 0] = i % 2 * 3.0 - 1.5
            x[:, g, 8] = digits
            x[:, g, 11, :, 0] = 2.0 ** -10
            u[:, h + 11, h, 0] = c
        elif i < 6: x[:, g, 8] = digits * rng.choice([-1.0, 1.0], (N, C, 1))
        else:
            x[:, g, 10, :, 0] = rng.choice([-1.0, 1.0], (N, C)) * 2.0 ** -30
            x[:, g, 11, :, 0] = 2.0 ** -29
            w[:, g, 10, 0, g, 9, 0] = 2.0 ** -9
            w[:, g, 12, 0, g, 9, 0] = 1.0
            w[:, g, 10, 0, g, 13, 0] = -2.0 ** -9
            w[:, g, 12, 0, g, 13, 0] = 1.0
            w[:, g, 11, 0, g, 11, 0] = 16.0
            u[:, h + 9, h, 0] = 1.125 * c
            u[:, h + 13, h, 0] = c
        if i < 6: u[:, h + 8, h] = c
        if i % 2: x[:, g, 0, at[i // 2], 0] = 2.0 ** 29 * rng.choice([-1.0, 1.0], N)
    return {"x": x.reshape(N, 128, 4 * C).astype(BF), "u": u.reshape(N, 128, 512), "v": d["v"], **stored(k, n), **weights(rng, w)}
def setup_inputs_odd(rng):
    d = numbers_of(rng)
    x = (1.0 + (2 * rng.integers(0, 64, (N, 16, 8, C, 4)) + 1) * 2.0 ** -7) * np.exp2(-rng.integers(0, 7, (N, 16, 8, C, 4)).astype(np.float64)) * rng.choice([-1.0, 1.0], (N, 16, 8, C, 4))
    x[:, :, 0, :, 0] = 1.96875 * 2.0 ** 8 * rng.choice([-1.0, 1.0], (N, 16, C))
    x[:, ::2, 1, :, 0] = (8 + rng.integers(0, 2, (N, 8, C))) * 2.0 ** -8
    u = d["u"].reshape(N, 128, 128, 4)
    u[:, :, ::16] = 0
    for h in range(0, 128, 16): u[:, h + 1, h, 0] = 1.0
    return {"x": x.astype(np.float32).reshape(N, 128, 4 * C).astype(BF), "u": u.reshape(N, 128, 512), "v": d["v"], **stored(*lists(rng)), **weights(rng, layers(rng, [0, 8]))}
def setup_inputs_ends(rng):
    d = numbers_of(rng)
    k, n = lists(rng)
    j = np.arange(C)
    o = np.zeros(N, np.int64)
    for i, r in enumerate(rng.permutation([r for r in range(N) if not r & MASK[0]])):
        o[r], o[r ^ MASK[0]] = rng.permutation([1, 2] if i % 2 else [0, 3])
    e, h = rng.permutation(N) % 4, rng.permutation(N) % 4
    k[e == 0] = j
    k[e == 1] = j[::-1]
    k[e == 2] = (j + 1) % C
    n[h == 0] = j[::-1]
    n[h == 1] = j ^ 1
    n[h == 2] = (j + C // 2) % C
    s = rng.choice([-1.0, 1.0], (N, 8, 16, C, 4))
    s[o == 0] = -1
    s[o == 1] = rng.choice([-1.0, 1.0], (N, 1, 1, C, 1))[o == 1]
    x = s * (0.955 + 0.02 * rng.random((N, 8, 16, C, 4))) * 2.0 ** 30
    x[o == 3] = 2.0 ** -30
    g = int(rng.integers(8))
    x[:, g, :8] = 2.0 ** -30
    size = np.where(o == 3, 2.0 ** -30, 2.0 ** 30)
    a = np.stack([rng.permutation(8) % 2 * 2.0 - 1.0 for r in range(N)]) * size[:, None]
    u = d["u"].reshape(N, 128, 128, 4)
    u[:, :, ::16] = a.astype(np.float32).astype(BF)[:, None, :, None]
    v = rng.choice([-1.0, 1.0], (N, 128, 512)) * size[:, None, None]
    w = np.zeros((N, 128, 4, 128, 4), np.float32)
    i, l = np.arange(128), np.arange(16 * g, 16 * g + 8)
    for b in range(4):
        w[:, i, b, i, b] = np.where(o == 3, 32.0, -0.125)[:, None]
        w[:, l, b, l, b] = np.where(o == 3, 256.0, 0.0)[:, None]
    return {"x": x.astype(np.float32).reshape(N, 128, 4 * C).astype(BF), "u": u.reshape(N, 128, 512), "v": v.astype(np.float32).astype(BF), **stored(k, n), **weights(rng, w.astype(BF))}
def setup_inputs_spread(rng):
    d = setup_inputs(rng)
    d["x"] = wide(rng, N, 128, 4 * C, cols=6)
    return d
def check_inputs(d):
    b = []
    for k in ("x", "u", "v"):
        a = np.abs(d[k].astype(np.float32))
        if not (np.isfinite(a).all() and ((a == 0) | (a >= 2.0 ** -30) & (a <= 2.0 ** 30)).all()): b.append("a value of " + k)
    none, least, most = [emit(mx_ref.quantize(np.full((128, 16), k, np.float32).astype(BF)))[1][0, 0] for k in (0.0, 2.0 ** -8, 2.0 ** 8)]
    top = emit(mx_ref.quantize(np.ascontiguousarray(np.tile(np.repeat(1.0 + np.arange(128) * 2.0 ** -7, 4), (128, 1))).astype(np.float32).astype(BF)))[0] & 0x7F
    for r in range(N):
        k, n = gentries(d["dl"][r]), gentries(d["nl"][r])
        if not (np.sort(k, axis=1) == np.arange(C)).all(): b.append("dl: not every column once")
        if not ((n >= 0) & (n < C)).all(): b.append("an entry of nl")
        elif not ((at(n, n) == np.arange(C)) & (n != np.arange(C))).all(): b.append("nl: not in pairs")
        if ((d["wc"][r] == 0x7F) | (d["wc"][r] == 0xFF)).any(): b.append("wc: a code that is no number")
        s = mx_ref.live(d["ws"][r])
        if ((s != none) & ((s < least) | (s > most))).any(): b.append("ws: a scale out of range")
        a = np.max(d["wc"][r].reshape(16, 8, 512, 4) & 0x7F, axis=(1, 3))
        if ((s == none) & (a != 0)).any(): b.append("wc: a code other than zero under the scale of zeros")
        if ((s != none) & ((a < top.min()) | (a > top.max()))).any(): b.append("wc: a block whose largest code isn't one of quantize_mx")
    return b
def at(t, e):
    return np.take_along_axis(t, e, axis=1)
def layer(w, q):
    return tile([mx_ref.matmul(pick(w, np.arange(128 * b, 128 * b + 128)), q) * np.float32(0.03125) for b in range(4)])
def reference(x, u, v, dl, nl, wc, ws):
    qu = [mx_ref.quantize(u[r]) for r in range(N)]
    lay = [pk(wc[r], ws[r]) for r in range(N)]
    d, n = [gentries(dl[r]) for r in range(N)], [gentries(nl[r]) for r in range(N)]
    now = [x[r] for r in range(N)]
    for m in MASK:
        s = [mx_ref.matmul(qu[r], mx_ref.quantize(now[r]))[::16] + np.float32(0.0) for r in range(N)]
        new, h, made = [], [], []
        for r in range(N):
            p = r ^ m
            a, b, k = np.tile(np.arange(C), (8, 1)), n[r], np.zeros((8, C), np.int64)
            for step in range(6):
                own = at(s[r], a) > at(s[p], b)
                a, b, k = np.where(own, at(d[r], a), a), np.where(own, b, at(d[p], b)), k + own
            z = ((gcols(now[r], a).astype(np.float32) + gcols(now[r], b).astype(np.float32)) * np.float32(0.5)).astype(BF)
            h.append(layer(lay[r], mx_ref.quantize(z)))
            new.append(np.where((k + at(k, n[r])) % 2 == 1, at(d[r], n[r]), d[r]))
        for r in range(N):
            p = r ^ m
            far = decode(mx_ref.quantize(np.ascontiguousarray(h[p][:, :4 * F]))).astype(BF)
            both = np.concatenate([far, h[r][:, 4 * F:]], axis=1)
            place = at(np.argsort(d[p], axis=1), new[r])
            made.append((now[r].astype(np.float32) + gcols(both, place).astype(np.float32)).astype(BF))
        now, d = made, new
    y, dn = np.zeros((N, 128, C), np.float32), np.zeros((N, 8, C), np.float32)
    oc, osc = np.zeros((N, 128, 4 * C), np.uint8), np.zeros((N, 16, C), np.uint8)
    for r in range(N):
        q = mx_ref.quantize(now[r])
        y[r] = mx_ref.matmul(mx_ref.quantize(v[r]), q)
        dn[r] = d[r]
        oc[r], osc[r] = emit(q)
    return {"y": y, "dn": dn, "oc": oc, "osc": osc}

@@ -1,0 +1,413 @@
+import numpy as np
+from concourse.bass import RemoteDMATransfer
+from concourse.mybir import dt, AluOpType as A, ActivationFunctionType as F
+
+C, FAR, HALF = 320, 240, 160
+MASKS = [4, 1, 2]
+HUGE = 2.0 ** 80
+UNIT = 2.0 ** 18
+
+f32, b16, i32, u16, q8, u8 = "float32", "bfloat16", "int32", "uint16", "float8_e4m3fn_x4", "uint8"
+SCRATCH = {
+    "xa": ("sbuf", [128, 4 * C], b16), "xb": ("sbuf", [128, 4 * C], b16),
+    "xh": ("sbuf", [128, 4 * C], b16), "zb": ("sbuf", [128, 4 * C], b16), "z": ("sbuf", [128, 4 * C], b16),
+    "h": ("sbuf", [128, 4 * C], b16), "j": ("sbuf", [128, 4 * C], b16),
+    "ut": ("sbuf", [128, 512], b16), "vt": ("sbuf", [128, 512], b16),
+    "ones": ("sbuf", [128, 512], b16), "eb": ("sbuf", [128, 2048], b16),
+    "qu": ("sbuf", [128, 128], q8), "pu": ("sbuf", [128, 128], u8),
+    "qr": ("sbuf", [128, 128], q8), "pr": ("sbuf", [128, 128], u8),
+    "qv": ("sbuf", [128, 128], q8), "pv": ("sbuf", [128, 128], u8),
+    "qe": ("sbuf", [128, 512], q8), "pe": ("sbuf", [128, 512], u8),
+    "qw": ("sbuf", [128, 512], q8), "pw": ("sbuf", [128, 512], u8),
+    "qx": ("sbuf", [128, C], q8), "px": ("sbuf", [128, C], u8),
+    "qz": ("sbuf", [128, C], q8), "pz": ("sbuf", [128, C], u8),
+    "dli": ("sbuf", [128, 20], i32), "nli": ("sbuf", [128, 20], i32),
+    "n_o": ("sbuf", [128, 20], u16), "f_o0": ("sbuf", [128, 20], u16),
+    "d_f0": ("sbuf", [128, 20], f32), "d_f1": ("sbuf", [128, 20], f32), "ddif": ("sbuf", [128, 20], f32),
+    "a_o": ("sbuf", [128, 20], u16), "b_o": ("sbuf", [128, 20], u16), "l_o": ("sbuf", [128, 20], u16),
+    "po": ("sbuf", [128, 20], i32), "ai": ("sbuf", [128, 20], i32), "bi": ("sbuf", [128, 20], i32),
+    "ki": ("sbuf", [128, 20], i32), "k2": ("sbuf", [128, 20], i32), "par": ("sbuf", [128, 20], i32),
+    "parf": ("sbuf", [128, 20], f32),
+    "ta": ("sbuf", [128, 24], f32), "tb": ("sbuf", [128, 24], f32),
+    "pidx": ("sbuf", [128, 1], i32), "sli": ("sbuf", [128, 1], i32), "hfi": ("sbuf", [128, 1], i32),
+    "rowi": ("sbuf", [128, 8], i32), "row_o": ("sbuf", [128, 8], u16),
+    "cst": ("sbuf", [128, 56], f32), "tv": ("sbuf", [128, 6], f32),
+    "iot": ("sbuf", [128, C], f32), "i512": ("sbuf", [128, C], f32), "cs": ("sbuf", [128, 672], f32),
+    "lt": ("sbuf", [128, C], f32), "v0": ("sbuf", [128, C], f32), "b0": ("sbuf", [128, C], f32),
+    "mask": ("sbuf", [128, C], f32), "seg": ("sbuf", [128, C], f32), "hold": ("sbuf", [128, C], f32),
+    "kt": ("sbuf", [128, 672], b16),
+    "ts": ("sbuf", [128, C], f32), "t1": ("sbuf", [128, C], f32), "sb": ("sbuf", [128, C], f32),
+    "va": ("sbuf", [128, C], f32), "vb": ("sbuf", [128, C], f32), "wa": ("sbuf", [128, C], f32), "wb": ("sbuf", [128, C], f32),
+    "te": ("sbuf", [128, C], f32), "bf": ("sbuf", [128, C], f32), "sbp": ("sbuf", [128, C], f32), "erow": ("sbuf", [128, C], f32),
+    "frow": ("sbuf", [128, C], f32), "einv": ("sbuf", [128, C], f32), "xm": ("sbuf", [128, C], f32), "xs": ("sbuf", [128, C], f32),
+    "irow": ("sbuf", [128, 352], b16), "irow2": ("sbuf", [128, 352], b16), "prow": ("sbuf", [128, 352], f32),
+    "tin": ("sbuf", [128, 672], b16), "tin2": ("sbuf", [128, 672], b16), "tp": ("sbuf", [128, 680], f32),
+    "sc": ("sbuf", [128, 672], f32), "sc2": ("sbuf", [128, 672], b16),
+}
+for _i in range(1, 7):
+    SCRATCH["yo%d" % _i] = ("sbuf", [128, C], f32)
+    SCRATCH["yp%d" % _i] = ("sbuf", [128, C], f32)
+for _r in range(3):
+    SCRATCH["ss%d" % _r] = ("sbuf", [128, 20], f32)
+    SCRATCH["sl%d" % _r] = ("sbuf", [128, 20], f32)
+    SCRATCH["el%d" % _r] = ("sbuf", [128, 20], u16)
+    SCRATCH["f_o%d" % (_r + 1)] = ("sbuf", [128, 20], u16)
+    SCRATCH["qh%d" % _r] = ("sbuf", [128, C], q8)
+    SCRATCH["ph%d" % _r] = ("sbuf", [128, C], u8)
+    SCRATCH["ql%d" % _r] = ("sbuf", [128, FAR], q8)
+    SCRATCH["pl%d" % _r] = ("sbuf", [128, FAR], u8)
+for _i in range(8):
+    SCRATCH["ps%d" % _i] = ("psum", [128, 512], f32)
+
+SEMAPHORES = ["sv", "sa", "st", "sg", "sent", "ldx", "ldu", "ldw", "ldv", "ldd", "ldn", "out"]
+for _r in range(3):
+    SEMAPHORES += ["s%d" % _r, "e%d" % _r, "ca%d" % _r, "cb%d" % _r, "cp%d" % _r]
+
+
+def rank_program(g, core, T, topo):
+    rank = T.rank_of(core)
+    if rank is None:
+        return
+    V, S, P, Y = g.vector, g.scalar, g.tensor, g.sync
+    queue = {"v": V, "s": S, "p": P, "y": Y, "g": g}
+    cnt = {"sv": 0, "sa": 0, "st": 0, "sg": 0, "sent": 0}
+    known = {}
+
+    def need(q, sem, n):
+        if known.get((q, sem), 0) < n:
+            queue[q].wait_ge(T.sem[sem], n)
+            known[(q, sem)] = n
+
+    def v(ins):
+        ins.then_inc(T.sem.sv, 1)
+        cnt["sv"] += 1
+        return cnt["sv"]
+
+    def s(ins):
+        ins.then_inc(T.sem.sa, 1)
+        cnt["sa"] += 1
+        return cnt["sa"]
+
+    def p(ins):
+        ins.then_inc(T.sem.st, 1)
+        cnt["st"] += 1
+        return cnt["st"]
+
+    def gc(ins):
+        ins.then_inc(T.sem.sg, 1)
+        cnt["sg"] += 1
+        return cnt["sg"]
+
+    def vv(n=None):
+        need("v", "sv", cnt["sv"] if n is None else n)
+
+    def peer(r):
+        return T.cores[rank ^ MASKS[r]]
+
+    def send(dst, out, in_, sem):
+        rid, pid = topo.addr(dst, core)
+        g.remote_dma(out, in_, T.sem[sem], T.sem.sent, pid, rid, topo.mask(core, dst))
+        cnt["sent"] += len(topo.engines(core, dst))
+
+    def landed(q, r, sem):
+        need(q, "%s%d" % (sem, r), len(topo.engines(peer(r), core)))
+
+    Y.dma_start(T.xa[:], T.x[:]).then_inc(T.sem.ldx, 16)
+    S.dma_start(T.dli[:], T.dl[:]).then_inc(T.sem.ldd, 16)
+    S.dma_start(T.ut[:], T.u[:]).then_inc(T.sem.ldu, 16)
+    S.dma_start(T.nli[:], T.nl[:]).then_inc(T.sem.ldn, 16)
+    Y.dma_start(T.qw[:].bitcast(dt.uint8), T.wc[:]).then_inc(T.sem.ldw, 16)
+    Y.dma_start(T.pw[:], T.ws[:]).then_inc(T.sem.ldw, 16)
+    Y.dma_start(T.vt[:], T.v[:]).then_inc(T.sem.ldv, 16)
+
+    gc(g.iota(T.pidx[:], [[0, 1]], 0, 1))
+    gc(g.iota(T.rowi[:], [[16, 8]], 0, 0))
+    g1 = gc(g.iota(T.tv[:], [[1, 6]], 1, 0, allow_small_or_imprecise_dtypes=True))
+    g2 = gc(g.iota(T.iot[:], [[1, C]], 0, 0, allow_small_or_imprecise_dtypes=True))
+
+    need("v", "ldd", 16)
+    v(V.tensor_copy(T.d_f0[:], T.dli[:]))
+    v0 = v(V.tensor_copy(T.f_o0[:], T.dli[:]))
+    need("g", "sv", v0)
+    send(peer(0), T.el0[:], T.f_o0[:], "e0")
+    g3 = gc(g.iota(T.cs[:], [[0, 42], [1, 16]], 0, 0, allow_small_or_imprecise_dtypes=True))
+    vo = v(V.memset(T.ones[:], 1.0))
+    need("g", "sv", vo)
+    for b in range(4):
+        g4 = gc(g.affine_select(T.eb[:, 512 * b:512 * b + 512], T.ones[:], [[-1, 512]], A.is_equal, 0.0, b, 4))
+
+    def col(k):
+        return T.cst[:, k:k + 1]
+    need("v", "sg", g1)
+    v(V.tensor_scalar(T.sli[:], T.pidx[:], 15, None, A.bitwise_and))
+    v(V.tensor_scalar(T.hfi[:], T.pidx[:], 16, None, A.bitwise_and))
+    v(V.tensor_copy(T.row_o[:], T.rowi[:]))
+    vv()
+    SLOT, M1, M0, GE1, LE6, MS, IS8, NB8, SL8, S7, S14, EQ14, LCC, GE9, LE14, IN9, GE8, LE13, IN8, S14B = range(20)
+    v(V.tensor_copy(col(SLOT), T.sli[:]))
+    v(V.tensor_scalar(col(M1), T.hfi[:], 0.0625, None, A.mult))
+    vv()
+    sl = col(SLOT)
+    v(V.tensor_scalar(col(M0), col(M1), -1.0, 1.0, A.mult, A.add))
+    v(V.tensor_scalar(col(GE1), sl, 1.0, None, A.is_ge))
+    v(V.tensor_scalar(col(LE6), sl, 6.0, None, A.is_le))
+    v(V.tensor_scalar(col(IS8), sl, 8.0, None, A.is_equal))
+    v(V.tensor_scalar(col(SL8), sl, 8.0, None, A.subtract))
+    v(V.tensor_scalar(col(S7), sl, -1.0, 7.0, A.mult, A.add))
+    v(V.tensor_scalar(col(S14), sl, -1.0, 14.0, A.mult, A.add))
+    v(V.tensor_scalar(col(EQ14), sl, 14.0, None, A.is_equal))
+    v(V.tensor_scalar(col(GE9), sl, 9.0, None, A.is_ge))
+    v(V.tensor_scalar(col(LE14), sl, 14.0, None, A.is_le))
+    v(V.tensor_scalar(col(GE8), sl, 8.0, 512.0, A.is_ge, A.mult))
+    v(V.tensor_scalar(col(LE13), sl, 13.0, None, A.is_le))
+    vv()
+    v(V.tensor_tensor(col(MS), col(GE1), col(LE6), A.mult))
+    v(V.tensor_tensor(col(IN9), col(GE9), col(LE14), A.mult))
+    v(V.tensor_tensor(col(IN8), col(GE8), col(LE13), A.mult))
+    v(V.tensor_tensor(col(S14B), col(S14), col(EQ14), A.add))
+    v(V.tensor_scalar(col(LCC), col(S14), UNIT, None, A.mult))
+    v(V.tensor_scalar(col(NB8), col(IS8), -HUGE, HUGE, A.mult, A.add))
+    tmp6, acto, actp, bio, bip = [T.cst[:, 24 + 6 * k:30 + 6 * k] for k in range(5)]
+    v(V.tensor_scalar(acto, T.tv[:], sl, col(GE1), A.is_ge, A.mult))
+    v(V.tensor_scalar(tmp6, T.tv[:], col(SL8), None, A.is_equal))
+    v(V.tensor_scalar(actp, T.tv[:], col(S7), col(LE6), A.is_ge, A.mult))
+    vv()
+    v(V.tensor_tensor(acto, acto, tmp6, A.add))
+    vv()
+    v(V.tensor_scalar(tmp6, T.tv[:], col(S14B), None, A.is_equal))
+    vv()
+    v(V.tensor_tensor(actp, actp, tmp6, A.add))
+    v(V.tensor_scalar(bio, acto, -HUGE, HUGE, A.mult, A.add))
+    vv()
+    v(V.tensor_scalar(bip, actp, -HUGE, HUGE, A.mult, A.add))
+    need("v", "sg", g2)
+    v(V.tensor_scalar(T.lt[:], T.iot[:], col(LCC), col(IN9), A.add, A.mult))
+    v(V.tensor_scalar(T.v0[:], T.iot[:], 6.0 * UNIT, col(IS8), A.add, A.mult))
+    v(V.tensor_scalar(T.bf[:], T.iot[:], col(IN8), None, A.mult))
+    v(V.tensor_scalar(T.i512[:], T.iot[:], 512.0, None, A.mult))
+    vv()
+    v(V.tensor_scalar(T.v0[:], T.v0[:], col(NB8), None, A.add))
+    v(V.transpose(T.b0[:], T.bf[:]))
+    need("v", "ldu", 16)
+    v(V.quantize_mx(T.qu[:], T.pu[:], T.ut[:]))
+    vv()
+    v(V.tensor_copy(T.qr[:].bitcast(dt.uint32), T.qu[:].bitcast(dt.uint32).indirect(T.row_o[:])))
+    vr = v(V.tensor_copy(T.pr[:], T.pu[:].indirect(T.row_o[:])))
+    need("v", "ldn", 16)
+    v(V.tensor_copy(T.n_o[:], T.nli[:]))
+    need("v", "ldx", 16)
+
+    X = [T.xa, T.xb, T.xa, T.xb]
+    ps = [T["ps%d" % i] for i in range(8)]
+
+    def scan_pick(src, out):
+        vv()
+        v(V.tensor_tensor_scan(T.xs[:], T.seg[:], src, 0.0, A.mult, A.add))
+        vv()
+        return v(V.tensor_copy(out, T.xs[:, 15:C:16]))
+
+    def to_offsets(sc, out):
+        vv()
+        v(V.tensor_scalar(T.ta[:, 0:21], sc[:, 6:672:32], col(M0), None, A.mult))
+        v(V.tensor_scalar(T.tb[:, 0:21], sc[:, 22:672:32], col(M1), None, A.mult))
+        vv()
+        v(V.tensor_tensor(out[:, 0:20:2], T.ta[:, 0:10], T.tb[:, 10:20], A.add))
+        return v(V.tensor_tensor(out[:, 1:20:2], T.ta[:, 11:21], T.tb[:, 0:10], A.add))
+
+    def mates_of(list_f):
+        vv()
+        v(V.tensor_tensor(T.xm[:], T.frow[:].indirect(T.n_o[:]), T.mask[:], A.mult))
+        scan_pick(T.xm[:], T.parf[:])
+        vv()
+        v(V.tensor_tensor(T.ddif[:], T.parf[:], list_f, A.subtract))
+
+    for r in range(3):
+        x, xn = X[r], X[r + 1]
+        d_o, e_o, f_o = T["f_o%d" % r], T["el%d" % r], T["f_o%d" % (r + 1)]
+        d_f, f_f = (T.d_f0, T.d_f1) if r % 2 == 0 else (T.d_f1, T.d_f0)
+        vv()
+        need("p", "sv", v(V.quantize_mx(T.qx[:], T.px[:], x[:])))
+        t = p(P.matmul_mx(ps[0][:, 0:C], T.qr[:], T.pr[:], T.qx[:], T.px[:], True, True))
+        need("v", "st", t)
+        vt = v(V.transpose(T.ts[:], ps[0][:, 0:C]))
+        vv()
+        need("g", "sv", v(V.tensor_copy(T["ss%d" % r][:], T.ts[:, 0:C:16])))
+        send(peer(r), T["sl%d" % r][:], T["ss%d" % r][:], "s%d" % r)
+        need("s", "sv", vt)
+        a1 = s(S.activation(T.t1[:], ps[0][:, 0:C], F.Copy, scale=col(MS)))
+        landed("s", r, "e")
+        a2 = s(S.activation(T.erow[:], T.i512[:].indirect(e_o[:]), F.Copy))
+        if r == 0:
+            need("v", "sg", g3)
+            v(V.tensor_scalar(T.mask[:], T.cs[:, 0:C], sl, None, A.is_equal))
+            v(V.tensor_scalar(T.seg[:], T.cs[:, 0:C], 0.0, None, A.not_equal))
+            v(V.tensor_scalar(T.hold[:], T.cs[:, 0:C], 2.0, None, A.is_ge))
+            v(V.tensor_scalar(T.te[:], T.cs[:, 0:C], 6.0, None, A.is_le))
+            v(V.tensor_scalar(T.kt[:], T.cs[:], -1.0, 6.0, A.mult, A.add))
+            v(V.memset(T.irow[:], 0.0))
+            v(V.memset(T.irow2[:], 0.0))
+            v(V.memset(T.prow[:], 0.0))
+            v(V.memset(T.tp[:], 0.0))
+            vv()
+            v(V.tensor_tensor(T.hold[:], T.hold[:], T.te[:], A.mult))
+        need("v", "sa", a1)
+        n = v(V.tensor_tensor(T.sb[:], T.t1[:], T.lt[:], A.add))
+        need("s", "sv", n)
+        ya = [s(S.activation(T["yo%d" % k][:], T.sb[:], F.Identity, bias=col(41 + k), scale=col(29 + k))) for k in range(1, 7)]
+        need("v", "sa", a2)
+        vv()
+        v(V.transpose(T.te[:], T.erow[:]))
+        vv()
+        v(V.tensor_copy(T.b0[:, 14:C:16], T.te[:, 0:C:16]))
+        win = T.v0
+        for k in range(1, 7):
+            need("v", "sa", ya[k - 1])
+            vv()
+            out = T.va if k % 2 else T.vb
+            v(V.tensor_tensor(out[:], win[:].indirect(d_o[:]), T["yo%d" % k][:], A.min))
+            win = out
+        own = win
+        for k in range(4):
+            s(S.activation(T.xh[:, C * k:C * k + C], x[:, k:4 * C:4], F.Copy, scale=0.5))
+        if r == 0:
+            n = s(S.activation(T.frow[:], T.iot[:].indirect(d_o[:]), F.Copy))
+            need("v", "sa", n)
+            mates_of(d_f[:])
+            need("v", "sg", g4)
+            v(V.quantize_mx(T.qe[:], T.pe[:], T.eb[:]))
+        landed("v", r, "s")
+        v(V.tensor_copy(T.b0[:, 1:C:16], T["sl%d" % r][:]))
+        vv()
+        v(V.tensor_tensor_scan(T.bf[:], T.hold[:], T.b0[:], 0.0, A.mult, A.add))
+        vv()
+        need("s", "sv", v(V.transpose(T.sbp[:], T.bf[:])))
+        ya = [s(S.activation(T["yp%d" % k][:], T.sbp[:], F.Identity, bias=col(47 + k), scale=col(35 + k))) for k in range(1, 7)]
+        win = T.yp1
+        landed("v", r, "e")
+        for k in range(2, 7):
+            need("v", "sa", ya[k - 1])
+            vv()
+            out = T.wa if k % 2 else T.wb
+            v(V.tensor_tensor(out[:], win[:].indirect(e_o[:]), T["yp%d" % k][:], A.min))
+            win = out
+        vv()
+        n1 = v(V.tensor_tensor(T.irow[:, 16:336], win[:].indirect(T.n_o[:]), own[:], A.is_lt))
+        n2 = v(V.tensor_tensor(T.prow[:, 16:336], win[:].indirect(T.n_o[:]), own[:], A.add))
+        vv(n1)
+        v(V.transpose(T.tin[:, 0:320], T.irow[:, 16:336]))
+        v(V.transpose(T.tin[:, 320:672], T.irow[:, 0:352]))
+        vv(n2)
+        v(V.transpose(T.tp[:, 0:320], T.prow[:, 16:336]))
+        v(V.transpose(T.tp[:, 320:672], T.prow[:, 0:352]))
+        vv()
+        v(V.tensor_tensor_scan(T.sc[:], T.tin[:], T.tp[:, 8:680], 0.0, A.mult, A.max))
+        to_offsets(T.sc, T.po)
+        vv()
+        n1 = v(V.tensor_scalar(T.bi[:], T.po[:], 9, 511, A.logical_shift_right, A.bitwise_and))
+        n2 = v(V.tensor_scalar(T.ai[:], T.po[:], 511, None, A.bitwise_and))
+        vv(n1)
+        nb = v(V.tensor_copy(T.b_o[:], T.bi[:]))
+        vv(n2)
+        na = v(V.tensor_copy(T.a_o[:], T.ai[:]))
+        need("s", "sv", nb)
+        za = [[s(S.activation(T.zb[:, C * k + HALF * h:C * k + HALF * h + HALF], T.xh[:, C * k:C * k + C].indirect(T.b_o[:, 10 * h:10 * h + 10]), F.Copy)) for k in range(4)] for h in range(2)]
+        tz = []
+        if r == 0:
+            need("p", "ldw", 32)
+        for h in range(2):
+            for k in range(4):
+                need("v", "sa", za[h][k])
+                vv(na)
+                v(V.tensor_tensor(T.z[:, 4 * HALF * h + k:4 * HALF * h + 4 * HALF:4], T.xh[:, C * k:C * k + C].indirect(T.a_o[:, 10 * h:10 * h + 10]), T.zb[:, C * k + HALF * h:C * k + HALF * h + HALF], A.add))
+            vv()
+            lo, hi = HALF * h, HALF * h + HALF
+            need("p", "sv", v(V.quantize_mx(T.qz[:, lo:hi], T.pz[:, lo:hi], T.z[:, 4 * lo:4 * hi])))
+            tz.append([p(P.matmul_mx(ps[4 * h + b][:, 0:HALF], T.qw[:, 128 * b:128 * b + 128], T.pw[:, 128 * b:128 * b + 128], T.qz[:, lo:hi], T.pz[:, lo:hi], True, True)) for b in range(4)])
+        qh, ph = T["qh%d" % r], T["ph%d" % r]
+        for b in range(4):
+            need("s", "st", tz[0][b])
+            ha = s(S.activation(T.h[:, b:4 * HALF:4], ps[b][:, 0:HALF], F.Copy, scale=0.03125))
+        for b in range(2):
+            need("s", "st", tz[1][b])
+            hb = s(S.activation(T.h[:, 4 * HALF + b:4 * C:4], ps[4 + b][:, 0:HALF], F.Copy, scale=0.03125))
+        need("v", "sa", ha)
+        n1 = v(V.quantize_mx(qh[:, 0:HALF], ph[:, 0:HALF], T.h[:, 0:4 * HALF]))
+        for b in range(2, 4):
+            need("v", "st", tz[1][b])
+            vb = v(V.tensor_scalar(T.h[:, 4 * HALF + b:4 * C:4], ps[4 + b][:, 0:HALF], 0.03125, None, A.mult))
+        need("v", "sa", hb)
+        vv()
+        n2 = v(V.quantize_mx(qh[:, HALF:C], ph[:, HALF:C], T.h[:, 4 * HALF:4 * C]))
+        need("g", "sv", n1)
+        send(peer(r), T["ql%d" % r][:, 0:HALF].bitcast(dt.uint8), qh[:, 0:HALF].bitcast(dt.uint8), "ca%d" % r)
+        need("g", "sv", n2)
+        send(peer(r), T["ql%d" % r][:, HALF:FAR].bitcast(dt.uint8), qh[:, HALF:FAR].bitcast(dt.uint8), "cb%d" % r)
+        send(peer(r), T["pl%d" % r][:, 0:FAR], ph[:, 0:FAR], "cp%d" % r)
+        for b in range(4):
+            if b == 2:
+                need("s", "sv", vb)
+            s(S.activation(T.j[:, C * b + FAR:C * b + C], ps[4 + b][:, FAR - HALF:HALF], F.Copy, scale=0.03125))
+        v(V.tensor_copy(T.irow2[:, 16:336], T.irow[:, 16:336].indirect(T.n_o[:])))
+        v(V.tensor_scalar(T.ki[:], T.po[:], 18, None, A.logical_shift_right))
+        vv()
+        v(V.transpose(T.tin2[:, 0:320], T.irow2[:, 16:336]))
+        v(V.transpose(T.tin2[:, 320:672], T.irow2[:, 0:352]))
+        vv()
+        v(V.tensor_tensor_scan(T.sc2[:], T.tin2[:], T.kt[:], 0.0, A.mult, A.max))
+        to_offsets(T.sc2, T.k2)
+        vv()
+        v(V.tensor_tensor(T.par[:], T.ki[:], T.k2[:], A.add))
+        vv()
+        v(V.tensor_scalar(T.par[:], T.par[:], 1, None, A.bitwise_and))
+        vv()
+        v(V.tensor_copy(T.parf[:], T.par[:]))
+        vv()
+        v(V.tensor_tensor(T.parf[:], T.parf[:], T.ddif[:], A.mult))
+        vv()
+        v(V.tensor_tensor(f_f[:], d_f[:], T.parf[:], A.add))
+        vv()
+        nf = v(V.tensor_copy(f_o[:], f_f[:]))
+        if r < 2:
+            need("g", "sv", nf)
+            send(peer(r + 1), T["el%d" % (r + 1)][:], f_o[:], "e%d" % (r + 1))
+        need("s", "sv", nf)
+        fr = s(S.activation(T.frow[:], T.iot[:].indirect(f_o[:]), F.Copy))
+        v(V.tensor_copy(T.einv[:].indirect(e_o[:]), T.iot[:]))
+        vv()
+        v(V.tensor_tensor(T.xm[:], T.einv[:].indirect(f_o[:]), T.mask[:], A.mult))
+        nl = scan_pick(T.xm[:], T.l_o[:])
+        if r < 2:
+            need("v", "sa", fr)
+            mates_of(f_f[:])
+        else:
+            need("y", "sa", fr)
+            Y.dma_start(T.dn[:], T.frow[0:128:16, :]).then_inc(T.sem.out, 16)
+        need("p", "sa", ha)
+        for k in ("ca", "cb", "cp"):
+            landed("p", r, k)
+        for b in range(4):
+            td = p(P.matmul_mx(ps[b][:, 0:FAR], T.qe[:, 128 * b:128 * b + 128], T.pe[:, 128 * b:128 * b + 128], T["ql%d" % r][:], T["pl%d" % r][:], True, True))
+            need("s", "st", td)
+            ja = s(S.activation(T.j[:, C * b:C * b + FAR], ps[b][:, 0:FAR], F.Copy))
+            need("v", "sa", ja)
+            vv(nl)
+            v(V.tensor_tensor(xn[:, b:4 * C:4], T.j[:, C * b:C * b + C].indirect(T.l_o[:]), x[:, b:4 * C:4], A.add))
+
+    need("v", "ldv", 16)
+    v(V.quantize_mx(T.qv[:], T.pv[:], T.vt[:]))
+    vv()
+    n = v(V.quantize_mx(T.qx[:], T.px[:], X[3][:]))
+    need("p", "sv", n)
+    t = p(P.matmul_mx(ps[0][:, 0:C], T.qv[:], T.pv[:], T.qx[:], T.px[:], True, True))
+    need("y", "sv", n)
+    need("s", "sv", n)
+    Y.dma_start(T.oc[:], T.qx[:].bitcast(dt.uint8)).then_inc(T.sem.out, 16)
+    for k in range(4):
+        (S if k % 2 else Y).dma_start(T.osc[4 * k:4 * k + 4, :], T.px[32 * k:32 * k + 4, :]).then_inc(T.sem.out, 16)
+    need("v", "st", t)
+    n = v(V.tensor_copy(T.ts[:], ps[0][:, 0:C]))
+    need("y", "sv", n)
+    Y.dma_start(T.y[:], T.ts[:]).then_inc(T.sem.out, 16)
+    g.wait_ge(T.sem.out, 16 * 7)
+    for k in ("sv", "sa", "st", "sg", "sent"):
+        need("g", k, cnt[k])

@@ -1,5 +1,4 @@
 import numpy as np
-from concourse.bass import RemoteDMATransfer
 from concourse.mybir import dt, AluOpType as A, ActivationFunctionType as F
 
 C, FAR, HALF = 320, 240, 160
@@ -25,28 +24,23 @@ SCRATCH = {
     "n_o": ("sbuf", [128, 20], u16), "f_o0": ("sbuf", [128, 20], u16),
     "d_f0": ("sbuf", [128, 20], f32), "d_f1": ("sbuf", [128, 20], f32), "ddif": ("sbuf", [128, 20], f32),
     "a_o": ("sbuf", [128, 20], u16), "b_o": ("sbuf", [128, 20], u16), "l_o": ("sbuf", [128, 20], u16),
-    "po": ("sbuf", [128, 20], i32), "ai": ("sbuf", [128, 20], i32), "bi": ("sbuf", [128, 20], i32),
-    "ki": ("sbuf", [128, 20], i32), "k2": ("sbuf", [128, 20], i32), "par": ("sbuf", [128, 20], i32),
-    "parf": ("sbuf", [128, 20], f32),
+    "ints": ("sbuf", [128, 120], i32),
+    "parf": ("sbuf", [128, 20], f32), "dnf": ("sbuf", [128, 20], f32),
     "ta": ("sbuf", [128, 24], f32), "tb": ("sbuf", [128, 24], f32),
     "pidx": ("sbuf", [128, 1], i32), "sli": ("sbuf", [128, 1], i32), "hfi": ("sbuf", [128, 1], i32),
     "rowi": ("sbuf", [128, 8], i32), "row_o": ("sbuf", [128, 8], u16),
-    "cst": ("sbuf", [128, 56], f32), "tv": ("sbuf", [128, 6], f32),
+    "cst": ("sbuf", [128, 24], f32), "tv": ("sbuf", [128, 6], f32),
     "iot": ("sbuf", [128, C], f32), "i512": ("sbuf", [128, C], f32), "cs": ("sbuf", [128, 672], f32),
-    "lt": ("sbuf", [128, C], f32), "v0": ("sbuf", [128, C], f32), "b0": ("sbuf", [128, C], f32),
     "mask": ("sbuf", [128, C], f32), "seg": ("sbuf", [128, C], f32), "hold": ("sbuf", [128, C], f32),
-    "kt": ("sbuf", [128, 672], b16),
-    "ts": ("sbuf", [128, C], f32), "t1": ("sbuf", [128, C], f32), "sb": ("sbuf", [128, C], f32),
-    "va": ("sbuf", [128, C], f32), "vb": ("sbuf", [128, C], f32), "wa": ("sbuf", [128, C], f32), "wb": ("sbuf", [128, C], f32),
-    "te": ("sbuf", [128, C], f32), "bf": ("sbuf", [128, C], f32), "sbp": ("sbuf", [128, C], f32), "erow": ("sbuf", [128, C], f32),
-    "frow": ("sbuf", [128, C], f32), "einv": ("sbuf", [128, C], f32), "xm": ("sbuf", [128, C], f32), "xs": ("sbuf", [128, C], f32),
+    "kt": ("sbuf", [128, 672], b16), "b0": ("sbuf", [128, C], f32),
+    "ts": ("sbuf", [128, C], f32), "bf": ("sbuf", [128, C], f32), "sbp": ("sbuf", [128, C], f32),
+    "tmt": ("sbuf", [128, C], f32), "tat": ("sbuf", [128, C], f32), "tbt": ("sbuf", [128, C], f32),
+    "wa": ("sbuf", [128, C], f32), "wb": ("sbuf", [128, C], f32), "m0": ("sbuf", [128, C], f32),
+    "einv": ("sbuf", [128, C], f32), "xm": ("sbuf", [128, C], f32), "xs": ("sbuf", [128, C], f32),
     "irow": ("sbuf", [128, 352], b16), "irow2": ("sbuf", [128, 352], b16), "prow": ("sbuf", [128, 352], f32),
-    "tin": ("sbuf", [128, 672], b16), "tin2": ("sbuf", [128, 672], b16), "tp": ("sbuf", [128, 680], f32),
+    "tin": ("sbuf", [128, 672], b16), "tin2": ("sbuf", [128, 672], b16), "tp": ("sbuf", [128, 672], f32),
     "sc": ("sbuf", [128, 672], f32), "sc2": ("sbuf", [128, 672], b16),
 }
-for _i in range(1, 7):
-    SCRATCH["yo%d" % _i] = ("sbuf", [128, C], f32)
-    SCRATCH["yp%d" % _i] = ("sbuf", [128, C], f32)
 for _r in range(3):
     SCRATCH["ss%d" % _r] = ("sbuf", [128, 20], f32)
     SCRATCH["sl%d" % _r] = ("sbuf", [128, 20], f32)
@@ -56,10 +50,13 @@ for _r in range(3):
     SCRATCH["ph%d" % _r] = ("sbuf", [128, C], u8)
     SCRATCH["ql%d" % _r] = ("sbuf", [128, FAR], q8)
     SCRATCH["pl%d" % _r] = ("sbuf", [128, FAR], u8)
+for _c in "mr", "ar", "br", "yp":
+    SCRATCH[_c + "a"] = ("sbuf", [128, 3 * C], f32)
+    SCRATCH[_c + "b"] = ("sbuf", [128, 3 * C], f32)
 for _i in range(8):
     SCRATCH["ps%d" % _i] = ("psum", [128, 512], f32)
 
-SEMAPHORES = ["sv", "sa", "st", "sg", "sent", "ldx", "ldu", "ldw", "ldv", "ldd", "ldn", "out"]
+SEMAPHORES = ["sv", "sa", "st", "sg", "sent", "ldx", "ldu", "ldw", "ldv", "ldd", "ldn", "out", "ta", "tb", "tm"]
 for _r in range(3):
     SEMAPHORES += ["s%d" % _r, "e%d" % _r, "ca%d" % _r, "cb%d" % _r, "cp%d" % _r]
 
@@ -70,7 +67,7 @@ def rank_program(g, core, T, topo):
         return
     V, S, P, Y = g.vector, g.scalar, g.tensor, g.sync
     queue = {"v": V, "s": S, "p": P, "y": Y, "g": g}
-    cnt = {"sv": 0, "sa": 0, "st": 0, "sg": 0, "sent": 0}
+    cnt = {"sv": 0, "sa": 0, "st": 0, "sg": 0, "sent": 0, "ta": 0, "tb": 0, "tm": 0}
     known = {}
 
     def need(q, sem, n):
@@ -78,25 +75,22 @@ def rank_program(g, core, T, topo):
             queue[q].wait_ge(T.sem[sem], n)
             known[(q, sem)] = n
 
+    def done(sem, ins, k=1):
+        ins.then_inc(T.sem[sem], k)
+        cnt[sem] += k
+        return cnt[sem]
+
     def v(ins):
-        ins.then_inc(T.sem.sv, 1)
-        cnt["sv"] += 1
-        return cnt["sv"]
+        return done("sv", ins)
 
     def s(ins):
-        ins.then_inc(T.sem.sa, 1)
-        cnt["sa"] += 1
-        return cnt["sa"]
+        return done("sa", ins)
 
     def p(ins):
-        ins.then_inc(T.sem.st, 1)
-        cnt["st"] += 1
-        return cnt["st"]
+        return done("st", ins)
 
     def gc(ins):
-        ins.then_inc(T.sem.sg, 1)
-        cnt["sg"] += 1
-        return cnt["sg"]
+        return done("sg", ins)
 
     def vv(n=None):
         need("v", "sv", cnt["sv"] if n is None else n)
@@ -112,6 +106,14 @@ def rank_program(g, core, T, topo):
     def landed(q, r, sem):
         need(q, "%s%d" % (sem, r), len(topo.engines(peer(r), core)))
 
+    def slot(sem, tile, i, src):
+        done(sem, Y.dma_start(tile[i:128:16, :], src), 16)
+
+    def rows(name, k, i=None):
+        lo = C * (k // 2)
+        buf = T[name + "ab"[k % 2]]
+        return buf[:, lo:lo + C] if i is None else buf[i:128:16, lo:lo + C]
+
     Y.dma_start(T.xa[:], T.x[:]).then_inc(T.sem.ldx, 16)
     S.dma_start(T.dli[:], T.dl[:]).then_inc(T.sem.ldd, 16)
     S.dma_start(T.ut[:], T.u[:]).then_inc(T.sem.ldu, 16)
@@ -125,78 +127,52 @@ def rank_program(g, core, T, topo):
     g1 = gc(g.iota(T.tv[:], [[1, 6]], 1, 0, allow_small_or_imprecise_dtypes=True))
     g2 = gc(g.iota(T.iot[:], [[1, C]], 0, 0, allow_small_or_imprecise_dtypes=True))
 
-    need("v", "ldd", 16)
-    v(V.tensor_copy(T.d_f0[:], T.dli[:]))
-    v0 = v(V.tensor_copy(T.f_o0[:], T.dli[:]))
-    need("g", "sv", v0)
-    send(peer(0), T.el0[:], T.f_o0[:], "e0")
-    g3 = gc(g.iota(T.cs[:], [[0, 42], [1, 16]], 0, 0, allow_small_or_imprecise_dtypes=True))
-    vo = v(V.memset(T.ones[:], 1.0))
-    need("g", "sv", vo)
-    for b in range(4):
-        g4 = gc(g.affine_select(T.eb[:, 512 * b:512 * b + 512], T.ones[:], [[-1, 512]], A.is_equal, 0.0, b, 4))
-
     def col(k):
         return T.cst[:, k:k + 1]
+    SLOT, M1, M0, LE6, S7 = range(5)
+    actp, bip = T.cst[:, 8:14], T.cst[:, 14:20]
+    v(V.memset(T.tat[:], 0.0))
+    ms = v(V.memset(T.tbt[:], 0.0))
     need("v", "sg", g1)
     v(V.tensor_scalar(T.sli[:], T.pidx[:], 15, None, A.bitwise_and))
     v(V.tensor_scalar(T.hfi[:], T.pidx[:], 16, None, A.bitwise_and))
     v(V.tensor_copy(T.row_o[:], T.rowi[:]))
     vv()
-    SLOT, M1, M0, GE1, LE6, MS, IS8, NB8, SL8, S7, S14, EQ14, LCC, GE9, LE14, IN9, GE8, LE13, IN8, S14B = range(20)
     v(V.tensor_copy(col(SLOT), T.sli[:]))
     v(V.tensor_scalar(col(M1), T.hfi[:], 0.0625, None, A.mult))
     vv()
     sl = col(SLOT)
     v(V.tensor_scalar(col(M0), col(M1), -1.0, 1.0, A.mult, A.add))
-    v(V.tensor_scalar(col(GE1), sl, 1.0, None, A.is_ge))
     v(V.tensor_scalar(col(LE6), sl, 6.0, None, A.is_le))
-    v(V.tensor_scalar(col(IS8), sl, 8.0, None, A.is_equal))
-    v(V.tensor_scalar(col(SL8), sl, 8.0, None, A.subtract))
     v(V.tensor_scalar(col(S7), sl, -1.0, 7.0, A.mult, A.add))
-    v(V.tensor_scalar(col(S14), sl, -1.0, 14.0, A.mult, A.add))
-    v(V.tensor_scalar(col(EQ14), sl, 14.0, None, A.is_equal))
-    v(V.tensor_scalar(col(GE9), sl, 9.0, None, A.is_ge))
-    v(V.tensor_scalar(col(LE14), sl, 14.0, None, A.is_le))
-    v(V.tensor_scalar(col(GE8), sl, 8.0, 512.0, A.is_ge, A.mult))
-    v(V.tensor_scalar(col(LE13), sl, 13.0, None, A.is_le))
     vv()
-    v(V.tensor_tensor(col(MS), col(GE1), col(LE6), A.mult))
-    v(V.tensor_tensor(col(IN9), col(GE9), col(LE14), A.mult))
-    v(V.tensor_tensor(col(IN8), col(GE8), col(LE13), A.mult))
-    v(V.tensor_tensor(col(S14B), col(S14), col(EQ14), A.add))
-    v(V.tensor_scalar(col(LCC), col(S14), UNIT, None, A.mult))
-    v(V.tensor_scalar(col(NB8), col(IS8), -HUGE, HUGE, A.mult, A.add))
-    tmp6, acto, actp, bio, bip = [T.cst[:, 24 + 6 * k:30 + 6 * k] for k in range(5)]
-    v(V.tensor_scalar(acto, T.tv[:], sl, col(GE1), A.is_ge, A.mult))
-    v(V.tensor_scalar(tmp6, T.tv[:], col(SL8), None, A.is_equal))
     v(V.tensor_scalar(actp, T.tv[:], col(S7), col(LE6), A.is_ge, A.mult))
     vv()
-    v(V.tensor_tensor(acto, acto, tmp6, A.add))
-    vv()
-    v(V.tensor_scalar(tmp6, T.tv[:], col(S14B), None, A.is_equal))
-    vv()
-    v(V.tensor_tensor(actp, actp, tmp6, A.add))
-    v(V.tensor_scalar(bio, acto, -HUGE, HUGE, A.mult, A.add))
-    vv()
     v(V.tensor_scalar(bip, actp, -HUGE, HUGE, A.mult, A.add))
+    need("v", "ldd", 16)
+    vd = v(V.tensor_copy(T.f_o0[:], T.dli[:]))
+    v(V.tensor_copy(T.d_f0[:], T.dli[:]))
+    need("g", "sv", vd)
+    send(peer(0), T.el0[:], T.f_o0[:], "e0")
+    g3 = gc(g.iota(T.cs[:], [[0, 42], [1, 16]], 0, 0, allow_small_or_imprecise_dtypes=True))
     need("v", "sg", g2)
-    v(V.tensor_scalar(T.lt[:], T.iot[:], col(LCC), col(IN9), A.add, A.mult))
-    v(V.tensor_scalar(T.v0[:], T.iot[:], 6.0 * UNIT, col(IS8), A.add, A.mult))
-    v(V.tensor_scalar(T.bf[:], T.iot[:], col(IN8), None, A.mult))
-    v(V.tensor_scalar(T.i512[:], T.iot[:], 512.0, None, A.mult))
-    vv()
-    v(V.tensor_scalar(T.v0[:], T.v0[:], col(NB8), None, A.add))
-    v(V.transpose(T.b0[:], T.bf[:]))
+    vi = v(V.tensor_scalar(T.i512[:], T.iot[:], 512.0, None, A.mult))
+    v(V.memset(T.tmt[:], HUGE))
+    v(V.memset(T.b0[:], 0.0))
     need("v", "ldu", 16)
     v(V.quantize_mx(T.qu[:], T.pu[:], T.ut[:]))
     vv()
     v(V.tensor_copy(T.qr[:].bitcast(dt.uint32), T.qu[:].bitcast(dt.uint32).indirect(T.row_o[:])))
-    vr = v(V.tensor_copy(T.pr[:], T.pu[:].indirect(T.row_o[:])))
+    v(V.tensor_copy(T.pr[:], T.pu[:].indirect(T.row_o[:])))
     need("v", "ldn", 16)
     v(V.tensor_copy(T.n_o[:], T.nli[:]))
+    need("y", "sg", g2)
+    need("y", "sv", vi)
+    slot("ta", T.tat, 6, T.iot[6:128:16, :])
+    slot("tb", T.tbt, 0, T.i512[0:128:16, :])
     need("v", "ldx", 16)
 
+    po_, ai_, bi_, ki_, k2_, par_ = [T.ints[:, 20 * k:20 * k + 20] for k in range(6)]
     X = [T.xa, T.xb, T.xa, T.xb]
     ps = [T["ps%d" % i] for i in range(8)]
 
@@ -211,15 +187,32 @@ def rank_program(g, core, T, topo):
         v(V.tensor_scalar(T.ta[:, 0:21], sc[:, 6:672:32], col(M0), None, A.mult))
         v(V.tensor_scalar(T.tb[:, 0:21], sc[:, 22:672:32], col(M1), None, A.mult))
         vv()
-        v(V.tensor_tensor(out[:, 0:20:2], T.ta[:, 0:10], T.tb[:, 10:20], A.add))
-        return v(V.tensor_tensor(out[:, 1:20:2], T.ta[:, 11:21], T.tb[:, 0:10], A.add))
+        v(V.tensor_tensor(T.ints[:, out:out + 20:2], T.ta[:, 0:10], T.tb[:, 10:20], A.add))
+        return v(V.tensor_tensor(T.ints[:, out + 1:out + 20:2], T.ta[:, 11:21], T.tb[:, 0:10], A.add))
 
-    def mates_of(list_f):
-        vv()
-        v(V.tensor_tensor(T.xm[:], T.frow[:].indirect(T.n_o[:]), T.mask[:], A.mult))
-        scan_pick(T.xm[:], T.parf[:])
-        vv()
-        v(V.tensor_tensor(T.ddif[:], T.parf[:], list_f, A.subtract))
+    def own_places(f_o, ks):
+        for k in ks:
+            win = T.iot[:] if k == 1 else rows("ar", k - 2)
+            if k > 1:
+                need("s", "sa", na_[0])
+            na_[0] = s(S.activation(rows("ar", k - 1), win.indirect(f_o[:]), F.Identity, bias=UNIT))
+            need("y", "sa", na_[0])
+            slot("ta", T.tat, 6 - k, rows("ar", k - 1, 6 - k))
+    na_ = [0]
+
+    def far_places(e_o, ks):
+        for k in ks:
+            win = T.i512[:] if k == 1 else rows("br", k - 2)
+            if k > 1:
+                need("s", "sa", nb_[0])
+            nb_[0] = s(S.activation(rows("br", k - 1), win.indirect(e_o[:]), F.Copy))
+            need("y", "sa", nb_[0])
+            slot("tb", T.tbt, k, rows("br", k - 1, k))
+    nb_ = [0]
+
+    need("s", "sg", g2)
+    need("s", "sv", vi)
+    own_places(T.f_o0, range(1, 7))
 
     for r in range(3):
         x, xn = X[r], X[r + 1]
@@ -227,88 +220,79 @@ def rank_program(g, core, T, topo):
         d_f, f_f = (T.d_f0, T.d_f1) if r % 2 == 0 else (T.d_f1, T.d_f0)
         vv()
         need("p", "sv", v(V.quantize_mx(T.qx[:], T.px[:], x[:])))
-        t = p(P.matmul_mx(ps[0][:, 0:C], T.qr[:], T.pr[:], T.qx[:], T.px[:], True, True))
-        need("v", "st", t)
-        vt = v(V.transpose(T.ts[:], ps[0][:, 0:C]))
+        t1 = p(P.matmul_mx(ps[0][:, 0:C], T.qr[:], T.pr[:], T.qx[:], T.px[:], True, True))
+        t2 = p(P.matmul_mx(ps[1][:, 0:C], T.qr[:], T.pr[:], T.qx[:], T.px[:], True, True))
+        need("v", "st", t1)
+        v(V.transpose(T.ts[:], ps[0][:, 0:C]))
         vv()
         need("g", "sv", v(V.tensor_copy(T["ss%d" % r][:], T.ts[:, 0:C:16])))
         send(peer(r), T["sl%d" % r][:], T["ss%d" % r][:], "s%d" % r)
-        need("s", "sv", vt)
-        a1 = s(S.activation(T.t1[:], ps[0][:, 0:C], F.Copy, scale=col(MS)))
+        need("s", "st", t2)
+        v(V.tensor_copy(T.m0[:], ps[0][:, 0:C]))
+        n = s(S.activation(rows("mr", 0), ps[1][:, 0:C], F.Copy))
         landed("s", r, "e")
-        a2 = s(S.activation(T.erow[:], T.i512[:].indirect(e_o[:]), F.Copy))
-        if r == 0:
-            need("v", "sg", g3)
-            v(V.tensor_scalar(T.mask[:], T.cs[:, 0:C], sl, None, A.is_equal))
-            v(V.tensor_scalar(T.seg[:], T.cs[:, 0:C], 0.0, None, A.not_equal))
-            v(V.tensor_scalar(T.hold[:], T.cs[:, 0:C], 2.0, None, A.is_ge))
-            v(V.tensor_scalar(T.te[:], T.cs[:, 0:C], 6.0, None, A.is_le))
-            v(V.tensor_scalar(T.kt[:], T.cs[:], -1.0, 6.0, A.mult, A.add))
-            v(V.memset(T.irow[:], 0.0))
-            v(V.memset(T.irow2[:], 0.0))
-            v(V.memset(T.prow[:], 0.0))
-            v(V.memset(T.tp[:], 0.0))
+        far_places(e_o, range(1, 7) if r == 0 else range(3, 7))
+        need("y", "sa", n)
+        slot("tm", T.tmt, 6, rows("mr", 0, 6))
+        need("v", "sa", n)
+        for k in range(1, 6):
             vv()
-            v(V.tensor_tensor(T.hold[:], T.hold[:], T.te[:], A.mult))
-        need("v", "sa", a1)
-        n = v(V.tensor_tensor(T.sb[:], T.t1[:], T.lt[:], A.add))
-        need("s", "sv", n)
-        ya = [s(S.activation(T["yo%d" % k][:], T.sb[:], F.Identity, bias=col(41 + k), scale=col(29 + k))) for k in range(1, 7)]
-        need("v", "sa", a2)
-        vv()
-        v(V.transpose(T.te[:], T.erow[:]))
-        vv()
-        v(V.tensor_copy(T.b0[:, 14:C:16], T.te[:, 0:C:16]))
-        win = T.v0
-        for k in range(1, 7):
-            need("v", "sa", ya[k - 1])
-            vv()
-            out = T.va if k % 2 else T.vb
-            v(V.tensor_tensor(out[:], win[:].indirect(d_o[:]), T["yo%d" % k][:], A.min))
-            win = out
-        own = win
+            n = v(V.tensor_tensor(rows("mr", k), rows("mr", k - 1).indirect(d_o[:]), T.m0[:], A.min))
+            need("y", "sv", n)
+            slot("tm", T.tmt, 6 - k, rows("mr", k, 6 - k))
         for k in range(4):
             s(S.activation(T.xh[:, C * k:C * k + C], x[:, k:4 * C:4], F.Copy, scale=0.5))
         if r == 0:
-            n = s(S.activation(T.frow[:], T.iot[:].indirect(d_o[:]), F.Copy))
-            need("v", "sa", n)
-            mates_of(d_f[:])
-            need("v", "sg", g4)
-            v(V.quantize_mx(T.qe[:], T.pe[:], T.eb[:]))
+            v(V.memset(T.ones[:], 1.0))
+            need("g", "sv", cnt["sv"])
+            for b in range(4):
+                g4 = gc(g.affine_select(T.eb[:, 512 * b:512 * b + 512], T.ones[:], [[-1, 512]], A.is_equal, 0.0, b, 4))
+            need("v", "sg", g3)
+            v(V.tensor_scalar(T.hold[:], T.cs[:, 0:C], 2.0, None, A.is_ge))
+            v(V.memset(T.irow[:], 0.0))
+            v(V.memset(T.prow[:], 0.0))
+            vv()
+        landed("v", r, "e")
+        v(V.tensor_copy(T.einv[:].indirect(e_o[:]), T.iot[:]))
+        need("v", "ta", cnt["ta"])
+        need("v", "tb", cnt["tb"])
+        v(V.tensor_tensor(T.prow[:, 16:336], T.tbt[:].indirect(T.n_o[:]), T.tat[:], A.add))
+        vv()
+        v(V.transpose(T.tp[:, 0:320], T.prow[:, 16:336]))
+        v(V.transpose(T.tp[:, 320:672], T.prow[:, 0:352]))
         landed("v", r, "s")
         v(V.tensor_copy(T.b0[:, 1:C:16], T["sl%d" % r][:]))
         vv()
         v(V.tensor_tensor_scan(T.bf[:], T.hold[:], T.b0[:], 0.0, A.mult, A.add))
         vv()
-        need("s", "sv", v(V.transpose(T.sbp[:], T.bf[:])))
-        ya = [s(S.activation(T["yp%d" % k][:], T.sbp[:], F.Identity, bias=col(47 + k), scale=col(35 + k))) for k in range(1, 7)]
-        win = T.yp1
-        landed("v", r, "e")
-        for k in range(2, 7):
+        n = v(V.transpose(T.sbp[:], T.bf[:]))
+        need("s", "sv", n)
+        ya = [s(S.activation(rows("yp", k), T.sbp[:], F.Identity, bias=bip[:, k:k + 1], scale=actp[:, k:k + 1])) for k in range(1, 6)]
+        vv()
+        v(V.tensor_scalar(rows("yp", 0), T.sbp[:], actp[:, 0:1], bip[:, 0:1], A.mult, A.add))
+        win = rows("yp", 0)
+        for k in range(1, 6):
             need("v", "sa", ya[k - 1])
             vv()
-            out = T.wa if k % 2 else T.wb
-            v(V.tensor_tensor(out[:], win[:].indirect(e_o[:]), T["yp%d" % k][:], A.min))
+            out = (T.wa if k % 2 else T.wb)[:]
+            v(V.tensor_tensor(out, win.indirect(e_o[:]), rows("yp", k), A.min))
             win = out
+        need("v", "tm", cnt["tm"])
         vv()
-        n1 = v(V.tensor_tensor(T.irow[:, 16:336], win[:].indirect(T.n_o[:]), own[:], A.is_lt))
-        n2 = v(V.tensor_tensor(T.prow[:, 16:336], win[:].indirect(T.n_o[:]), own[:], A.add))
-        vv(n1)
+        v(V.tensor_tensor(T.irow[:, 16:336], win.indirect(T.n_o[:]), T.tmt[:], A.is_lt))
+        vv()
         v(V.transpose(T.tin[:, 0:320], T.irow[:, 16:336]))
-        v(V.transpose(T.tin[:, 320:672], T.irow[:, 0:352]))
-        vv(n2)
-        v(V.transpose(T.tp[:, 0:320], T.prow[:, 16:336]))
-        v(V.transpose(T.tp[:, 320:672], T.prow[:, 0:352]))
+        nir = v(V.transpose(T.tin[:, 320:672], T.irow[:, 0:352]))
         vv()
-        v(V.tensor_tensor_scan(T.sc[:], T.tin[:], T.tp[:, 8:680], 0.0, A.mult, A.max))
-        to_offsets(T.sc, T.po)
+        v(V.tensor_tensor_scan(T.sc[:], T.tin[:], T.tp[:], 0.0, A.mult, A.max))
+        to_offsets(T.sc, 0)
         vv()
-        n1 = v(V.tensor_scalar(T.bi[:], T.po[:], 9, 511, A.logical_shift_right, A.bitwise_and))
-        n2 = v(V.tensor_scalar(T.ai[:], T.po[:], 511, None, A.bitwise_and))
+        n1 = v(V.tensor_scalar(bi_, po_, 9, 511, A.logical_shift_right, A.bitwise_and))
+        n2 = v(V.tensor_scalar(ai_, po_, 511, None, A.bitwise_and))
         vv(n1)
-        nb = v(V.tensor_copy(T.b_o[:], T.bi[:]))
+        nb = v(V.tensor_copy(T.b_o[:], bi_))
         vv(n2)
-        na = v(V.tensor_copy(T.a_o[:], T.ai[:]))
+        na = v(V.tensor_copy(T.a_o[:], ai_))
         need("s", "sv", nb)
         za = [[s(S.activation(T.zb[:, C * k + HALF * h:C * k + HALF * h + HALF], T.xh[:, C * k:C * k + C].indirect(T.b_o[:, 10 * h:10 * h + 10]), F.Copy)) for k in range(4)] for h in range(2)]
         tz = []
@@ -343,24 +327,39 @@ def rank_program(g, core, T, topo):
         need("g", "sv", n2)
         send(peer(r), T["ql%d" % r][:, HALF:FAR].bitcast(dt.uint8), qh[:, HALF:FAR].bitcast(dt.uint8), "cb%d" % r)
         send(peer(r), T["pl%d" % r][:, 0:FAR], ph[:, 0:FAR], "cp%d" % r)
+        if r == 0:
+            v(V.memset(T.irow2[:], 0.0))
+            vv()
+            need("s", "sv", cnt["sv"])
+        ni = s(S.activation(T.irow2[:, 16:336], T.irow[:, 16:336].indirect(T.n_o[:]), F.Copy))
         for b in range(4):
             if b == 2:
                 need("s", "sv", vb)
             s(S.activation(T.j[:, C * b + FAR:C * b + C], ps[4 + b][:, FAR - HALF:HALF], F.Copy, scale=0.03125))
-        v(V.tensor_copy(T.irow2[:, 16:336], T.irow[:, 16:336].indirect(T.n_o[:])))
-        v(V.tensor_scalar(T.ki[:], T.po[:], 18, None, A.logical_shift_right))
-        vv()
+        v(V.tensor_scalar(ki_, po_, 18, None, A.logical_shift_right))
+        if r == 0:
+            v(V.tensor_scalar(T.mask[:], T.cs[:, 0:C], sl, None, A.is_equal))
+            v(V.tensor_scalar(T.seg[:], T.cs[:, 0:C], 1.0, None, A.is_ge))
+            v(V.tensor_scalar(T.kt[:], T.cs[:], -1.0, 6.0, A.mult, A.add))
+            vv()
+            v(V.tensor_tensor(T.xm[:], rows("ar", 0).indirect(T.n_o[:]), T.mask[:], A.mult))
+            scan_pick(T.xm[:], T.parf[:])
+            vv()
+            v(V.tensor_scalar(T.dnf[:], T.parf[:], UNIT, None, A.subtract))
+            vv()
+            v(V.tensor_tensor(T.ddif[:], T.dnf[:], d_f[:], A.subtract))
+        need("v", "sa", ni)
         v(V.transpose(T.tin2[:, 0:320], T.irow2[:, 16:336]))
         v(V.transpose(T.tin2[:, 320:672], T.irow2[:, 0:352]))
         vv()
         v(V.tensor_tensor_scan(T.sc2[:], T.tin2[:], T.kt[:], 0.0, A.mult, A.max))
-        to_offsets(T.sc2, T.k2)
+        to_offsets(T.sc2, 80)
         vv()
-        v(V.tensor_tensor(T.par[:], T.ki[:], T.k2[:], A.add))
+        v(V.tensor_tensor(par_, ki_, k2_, A.add))
         vv()
-        v(V.tensor_scalar(T.par[:], T.par[:], 1, None, A.bitwise_and))
+        v(V.tensor_scalar(par_, par_, 1, None, A.bitwise_and))
         vv()
-        v(V.tensor_copy(T.parf[:], T.par[:]))
+        v(V.tensor_copy(T.parf[:], par_))
         vv()
         v(V.tensor_tensor(T.parf[:], T.parf[:], T.ddif[:], A.mult))
         vv()
@@ -370,19 +369,28 @@ def rank_program(g, core, T, topo):
         if r < 2:
             need("g", "sv", nf)
             send(peer(r + 1), T["el%d" % (r + 1)][:], f_o[:], "e%d" % (r + 1))
-        need("s", "sv", nf)
-        fr = s(S.activation(T.frow[:], T.iot[:].indirect(f_o[:]), F.Copy))
-        v(V.tensor_copy(T.einv[:].indirect(e_o[:]), T.iot[:]))
         vv()
         v(V.tensor_tensor(T.xm[:], T.einv[:].indirect(f_o[:]), T.mask[:], A.mult))
         nl = scan_pick(T.xm[:], T.l_o[:])
+        need("s", "sv", nf)
         if r < 2:
-            need("v", "sa", fr)
-            mates_of(f_f[:])
+            own_places(f_o, range(1, 5))
+            v(V.tensor_scalar(T.dnf[:], T.parf[:], -2.0, None, A.mult))
+            vv()
+            v(V.tensor_tensor(T.ddif[:], T.ddif[:], T.dnf[:], A.add))
         else:
-            need("y", "sa", fr)
-            Y.dma_start(T.dn[:], T.frow[0:128:16, :]).then_inc(T.sem.out, 16)
+            n = s(S.activation(rows("ar", 0), T.iot[:].indirect(f_o[:]), F.Copy))
+            need("y", "sa", n)
+            Y.dma_start(T.dn[:], rows("ar", 0, 0)).then_inc(T.sem.out, 16)
+        if r == 0:
+            need("v", "sg", g4)
+            v(V.quantize_mx(T.qe[:], T.pe[:], T.eb[:]))
+            need("p", "sv", cnt["sv"])
+        if r == 1:
+            need("v", "ldv", 16)
+            v(V.quantize_mx(T.qv[:], T.pv[:], T.vt[:]))
         need("p", "sa", ha)
+        need("p", "sv", vb)
         for k in ("ca", "cb", "cp"):
             landed("p", r, k)
         for b in range(4):
@@ -392,9 +400,11 @@ def rank_program(g, core, T, topo):
             need("v", "sa", ja)
             vv(nl)
             v(V.tensor_tensor(xn[:, b:4 * C:4], T.j[:, C * b:C * b + C].indirect(T.l_o[:]), x[:, b:4 * C:4], A.add))
+        if r < 2:
+            own_places(f_o, range(5, 7))
+            landed("s", r + 1, "e")
+            far_places(T["el%d" % (r + 1)], range(1, 3))
 
-    need("v", "ldv", 16)
-    v(V.quantize_mx(T.qv[:], T.pv[:], T.vt[:]))
     vv()
     n = v(V.quantize_mx(T.qx[:], T.px[:], X[3][:]))
     need("p", "sv", n)
@@ -409,5 +419,5 @@ def rank_program(g, core, T, topo):
     need("y", "sv", n)
     Y.dma_start(T.y[:], T.ts[:]).then_inc(T.sem.out, 16)
     g.wait_ge(T.sem.out, 16 * 7)
-    for k in ("sv", "sa", "st", "sg", "sent"):
+    for k in ("sv", "sa", "st", "sg", "sent", "ta", "tb", "tm"):
         need("g", k, cnt[k])

import numpy as np
from concourse.mybir import dt, AluOpType as A, ActivationFunctionType as F

C, FAR, HALF = 320, 240, 160
MASKS = [4, 1, 2]
HUGE = 2.0 ** 80
UNIT = 2.0 ** 18

f32, b16, i32, u16, q8, u8 = "float32", "bfloat16", "int32", "uint16", "float8_e4m3fn_x4", "uint8"
SCRATCH = {
    "xa": ("sbuf", [128, 4 * C], b16), "xb": ("sbuf", [128, 4 * C], b16),
    "xh": ("sbuf", [128, 4 * C], b16), "zb": ("sbuf", [128, 4 * C], b16), "z": ("sbuf", [128, 4 * C], b16),
    "h": ("sbuf", [128, 4 * C], b16), "j": ("sbuf", [128, 4 * C], b16),
    "ut": ("sbuf", [128, 512], b16), "vt": ("sbuf", [128, 512], b16),
    "ones": ("sbuf", [128, 512], b16), "eb": ("sbuf", [128, 2048], b16),
    "qu": ("sbuf", [128, 128], q8), "pu": ("sbuf", [128, 128], u8),
    "qr": ("sbuf", [128, 128], q8), "pr": ("sbuf", [128, 128], u8),
    "qv": ("sbuf", [128, 128], q8), "pv": ("sbuf", [128, 128], u8),
    "qe": ("sbuf", [128, 512], q8), "pe": ("sbuf", [128, 512], u8),
    "qw": ("sbuf", [128, 512], q8), "pw": ("sbuf", [128, 512], u8),
    "qx": ("sbuf", [128, C], q8), "px": ("sbuf", [128, C], u8),
    "qz": ("sbuf", [128, C], q8), "pz": ("sbuf", [128, C], u8),
    "dli": ("sbuf", [128, 20], i32), "nli": ("sbuf", [128, 20], i32),
    "n_o": ("sbuf", [128, 20], u16), "f_o0": ("sbuf", [128, 20], u16),
    "d_f0": ("sbuf", [128, 20], f32), "d_f1": ("sbuf", [128, 20], f32), "ddif": ("sbuf", [128, 20], f32),
    "a_o": ("sbuf", [128, 20], u16), "b_o": ("sbuf", [128, 20], u16), "l_o": ("sbuf", [128, 20], u16),
    "ints": ("sbuf", [128, 120], i32),
    "parf": ("sbuf", [128, 20], f32), "dnf": ("sbuf", [128, 20], f32),
    "ta": ("sbuf", [128, 24], f32), "tb": ("sbuf", [128, 24], f32),
    "pidx": ("sbuf", [128, 1], i32), "sli": ("sbuf", [128, 1], i32), "hfi": ("sbuf", [128, 1], i32),
    "rowi": ("sbuf", [128, 8], i32), "row_o": ("sbuf", [128, 8], u16),
    "cst": ("sbuf", [128, 24], f32), "tv": ("sbuf", [128, 6], f32),
    "iot": ("sbuf", [128, C], f32), "i512": ("sbuf", [128, C], f32), "cs": ("sbuf", [128, 672], f32),
    "mask": ("sbuf", [128, C], f32), "seg": ("sbuf", [128, C], f32), "hold": ("sbuf", [128, C], f32),
    "kt": ("sbuf", [128, 672], b16), "b0": ("sbuf", [128, C], f32),
    "ts": ("sbuf", [128, C], f32), "bf": ("sbuf", [128, C], f32), "sbp": ("sbuf", [128, C], f32),
    "tmt": ("sbuf", [128, C], f32), "tat": ("sbuf", [128, C], f32), "tbt": ("sbuf", [128, C], f32),
    "wa": ("sbuf", [128, C], f32), "wb": ("sbuf", [128, C], f32), "m0": ("sbuf", [128, C], f32),
    "einv": ("sbuf", [128, C], f32), "xm": ("sbuf", [128, C], f32), "xs": ("sbuf", [128, C], f32),
    "irow": ("sbuf", [128, 352], b16), "irow2": ("sbuf", [128, 352], b16), "prow": ("sbuf", [128, 352], f32),
    "tin": ("sbuf", [128, 672], b16), "tin2": ("sbuf", [128, 672], b16), "tp": ("sbuf", [128, 672], f32),
    "sc": ("sbuf", [128, 672], f32), "sc2": ("sbuf", [128, 672], b16),
}
for _r in range(3):
    SCRATCH["ss%d" % _r] = ("sbuf", [128, 20], f32)
    SCRATCH["sl%d" % _r] = ("sbuf", [128, 20], f32)
    SCRATCH["el%d" % _r] = ("sbuf", [128, 20], u16)
    SCRATCH["f_o%d" % (_r + 1)] = ("sbuf", [128, 20], u16)
    SCRATCH["qh%d" % _r] = ("sbuf", [128, C], q8)
    SCRATCH["ph%d" % _r] = ("sbuf", [128, C], u8)
    SCRATCH["ql%d" % _r] = ("sbuf", [128, FAR], q8)
    SCRATCH["pl%d" % _r] = ("sbuf", [128, FAR], u8)
for _c in "mr", "ar", "br", "yp":
    SCRATCH[_c + "a"] = ("sbuf", [128, 3 * C], f32)
    SCRATCH[_c + "b"] = ("sbuf", [128, 3 * C], f32)
for _i in range(8):
    SCRATCH["ps%d" % _i] = ("psum", [128, 512], f32)

SEMAPHORES = ["sv", "sa", "st", "sg", "sent", "ldx", "ldu", "ldw", "ldv", "ldd", "ldn", "out", "ta", "tb", "tm"]
for _r in range(3):
    SEMAPHORES += ["s%d" % _r, "e%d" % _r, "ca%d" % _r, "cb%d" % _r, "cp%d" % _r]


def rank_program(g, core, T, topo):
    rank = T.rank_of(core)
    if rank is None:
        return
    V, S, P, Y = g.vector, g.scalar, g.tensor, g.sync
    queue = {"v": V, "s": S, "p": P, "y": Y, "g": g}
    cnt = {"sv": 0, "sa": 0, "st": 0, "sg": 0, "sent": 0, "ta": 0, "tb": 0, "tm": 0}
    known = {}

    def need(q, sem, n):
        if known.get((q, sem), 0) < n:
            queue[q].wait_ge(T.sem[sem], n)
            known[(q, sem)] = n

    def done(sem, ins, k=1):
        ins.then_inc(T.sem[sem], k)
        cnt[sem] += k
        return cnt[sem]

    def v(ins):
        return done("sv", ins)

    def s(ins):
        return done("sa", ins)

    def p(ins):
        return done("st", ins)

    def gc(ins):
        return done("sg", ins)

    def vv(n=None):
        need("v", "sv", cnt["sv"] if n is None else n)

    def peer(r):
        return T.cores[rank ^ MASKS[r]]

    def send(dst, out, in_, sem):
        rid, pid = topo.addr(dst, core)
        g.remote_dma(out, in_, T.sem[sem], T.sem.sent, pid, rid, topo.mask(core, dst))
        cnt["sent"] += len(topo.engines(core, dst))

    def landed(q, r, sem):
        need(q, "%s%d" % (sem, r), len(topo.engines(peer(r), core)))

    def slot(sem, tile, i, src):
        done(sem, Y.dma_start(tile[i:128:16, :], src), 16)

    def rows(name, k, i=None):
        lo = C * (k // 2)
        buf = T[name + "ab"[k % 2]]
        return buf[:, lo:lo + C] if i is None else buf[i:128:16, lo:lo + C]

    Y.dma_start(T.xa[:], T.x[:]).then_inc(T.sem.ldx, 16)
    S.dma_start(T.dli[:], T.dl[:]).then_inc(T.sem.ldd, 16)
    S.dma_start(T.ut[:], T.u[:]).then_inc(T.sem.ldu, 16)
    S.dma_start(T.nli[:], T.nl[:]).then_inc(T.sem.ldn, 16)
    Y.dma_start(T.qw[:].bitcast(dt.uint8), T.wc[:]).then_inc(T.sem.ldw, 16)
    Y.dma_start(T.pw[:], T.ws[:]).then_inc(T.sem.ldw, 16)
    Y.dma_start(T.vt[:], T.v[:]).then_inc(T.sem.ldv, 16)

    gc(g.iota(T.pidx[:], [[0, 1]], 0, 1))
    gc(g.iota(T.rowi[:], [[16, 8]], 0, 0))
    g1 = gc(g.iota(T.tv[:], [[1, 6]], 1, 0, allow_small_or_imprecise_dtypes=True))
    g2 = gc(g.iota(T.iot[:], [[1, C]], 0, 0, allow_small_or_imprecise_dtypes=True))

    def col(k):
        return T.cst[:, k:k + 1]
    SLOT, M1, M0, LE6, S7 = range(5)
    actp, bip = T.cst[:, 8:14], T.cst[:, 14:20]
    v(V.memset(T.tat[:], 0.0))
    ms = v(V.memset(T.tbt[:], 0.0))
    need("v", "sg", g1)
    v(V.tensor_scalar(T.sli[:], T.pidx[:], 15, None, A.bitwise_and))
    v(V.tensor_scalar(T.hfi[:], T.pidx[:], 16, None, A.bitwise_and))
    v(V.tensor_copy(T.row_o[:], T.rowi[:]))
    vv()
    v(V.tensor_copy(col(SLOT), T.sli[:]))
    v(V.tensor_scalar(col(M1), T.hfi[:], 0.0625, None, A.mult))
    vv()
    sl = col(SLOT)
    v(V.tensor_scalar(col(M0), col(M1), -1.0, 1.0, A.mult, A.add))
    v(V.tensor_scalar(col(LE6), sl, 6.0, None, A.is_le))
    v(V.tensor_scalar(col(S7), sl, -1.0, 7.0, A.mult, A.add))
    vv()
    v(V.tensor_scalar(actp, T.tv[:], col(S7), col(LE6), A.is_ge, A.mult))
    vv()
    v(V.tensor_scalar(bip, actp, -HUGE, HUGE, A.mult, A.add))
    need("v", "ldd", 16)
    vd = v(V.tensor_copy(T.f_o0[:], T.dli[:]))
    v(V.tensor_copy(T.d_f0[:], T.dli[:]))
    need("g", "sv", vd)
    send(peer(0), T.el0[:], T.f_o0[:], "e0")
    g3 = gc(g.iota(T.cs[:], [[0, 42], [1, 16]], 0, 0, allow_small_or_imprecise_dtypes=True))
    need("v", "sg", g2)
    vi = v(V.tensor_scalar(T.i512[:], T.iot[:], 512.0, None, A.mult))
    v(V.memset(T.tmt[:], HUGE))
    v(V.memset(T.b0[:], 0.0))
    need("v", "ldu", 16)
    v(V.quantize_mx(T.qu[:], T.pu[:], T.ut[:]))
    vv()
    v(V.tensor_copy(T.qr[:].bitcast(dt.uint32), T.qu[:].bitcast(dt.uint32).indirect(T.row_o[:])))
    v(V.tensor_copy(T.pr[:], T.pu[:].indirect(T.row_o[:])))
    need("v", "ldn", 16)
    v(V.tensor_copy(T.n_o[:], T.nli[:]))
    need("y", "sg", g2)
    need("y", "sv", vi)
    slot("ta", T.tat, 6, T.iot[6:128:16, :])
    slot("tb", T.tbt, 0, T.i512[0:128:16, :])
    need("v", "ldx", 16)

    po_, ai_, bi_, ki_, k2_, par_ = [T.ints[:, 20 * k:20 * k + 20] for k in range(6)]
    X = [T.xa, T.xb, T.xa, T.xb]
    ps = [T["ps%d" % i] for i in range(8)]

    def scan_pick(src, out):
        vv()
        v(V.tensor_tensor_scan(T.xs[:], T.seg[:], src, 0.0, A.mult, A.add))
        vv()
        return v(V.tensor_copy(out, T.xs[:, 15:C:16]))

    def to_offsets(sc, out):
        vv()
        v(V.tensor_scalar(T.ta[:, 0:21], sc[:, 6:672:32], col(M0), None, A.mult))
        v(V.tensor_scalar(T.tb[:, 0:21], sc[:, 22:672:32], col(M1), None, A.mult))
        vv()
        v(V.tensor_tensor(T.ints[:, out:out + 20:2], T.ta[:, 0:10], T.tb[:, 10:20], A.add))
        return v(V.tensor_tensor(T.ints[:, out + 1:out + 20:2], T.ta[:, 11:21], T.tb[:, 0:10], A.add))

    def own_places(f_o, ks):
        for k in ks:
            win = T.iot[:] if k == 1 else rows("ar", k - 2)
            if k > 1:
                need("s", "sa", na_[0])
            na_[0] = s(S.activation(rows("ar", k - 1), win.indirect(f_o[:]), F.Identity, bias=UNIT))
            need("y", "sa", na_[0])
            slot("ta", T.tat, 6 - k, rows("ar", k - 1, 6 - k))
    na_ = [0]

    def far_places(e_o, ks):
        for k in ks:
            win = T.i512[:] if k == 1 else rows("br", k - 2)
            if k > 1:
                need("s", "sa", nb_[0])
            nb_[0] = s(S.activation(rows("br", k - 1), win.indirect(e_o[:]), F.Copy))
            need("y", "sa", nb_[0])
            slot("tb", T.tbt, k, rows("br", k - 1, k))
    nb_ = [0]

    need("s", "sg", g2)
    need("s", "sv", vi)
    own_places(T.f_o0, range(1, 7))

    for r in range(3):
        x, xn = X[r], X[r + 1]
        d_o, e_o, f_o = T["f_o%d" % r], T["el%d" % r], T["f_o%d" % (r + 1)]
        d_f, f_f = (T.d_f0, T.d_f1) if r % 2 == 0 else (T.d_f1, T.d_f0)
        vv()
        need("p", "sv", v(V.quantize_mx(T.qx[:], T.px[:], x[:])))
        t1 = p(P.matmul_mx(ps[0][:, 0:C], T.qr[:], T.pr[:], T.qx[:], T.px[:], True, True))
        t2 = p(P.matmul_mx(ps[1][:, 0:C], T.qr[:], T.pr[:], T.qx[:], T.px[:], True, True))
        need("v", "st", t1)
        v(V.transpose(T.ts[:], ps[0][:, 0:C]))
        vv()
        need("g", "sv", v(V.tensor_copy(T["ss%d" % r][:], T.ts[:, 0:C:16])))
        send(peer(r), T["sl%d" % r][:], T["ss%d" % r][:], "s%d" % r)
        need("s", "st", t2)
        v(V.tensor_copy(T.m0[:], ps[0][:, 0:C]))
        n = s(S.activation(rows("mr", 0), ps[1][:, 0:C], F.Copy))
        landed("s", r, "e")
        far_places(e_o, range(1, 7) if r == 0 else range(3, 7))
        need("y", "sa", n)
        slot("tm", T.tmt, 6, rows("mr", 0, 6))
        need("v", "sa", n)
        for k in range(1, 6):
            vv()
            n = v(V.tensor_tensor(rows("mr", k), rows("mr", k - 1).indirect(d_o[:]), T.m0[:], A.min))
            need("y", "sv", n)
            slot("tm", T.tmt, 6 - k, rows("mr", k, 6 - k))
        for k in range(4):
            s(S.activation(T.xh[:, C * k:C * k + C], x[:, k:4 * C:4], F.Copy, scale=0.5))
        if r == 0:
            v(V.memset(T.ones[:], 1.0))
            need("g", "sv", cnt["sv"])
            for b in range(4):
                g4 = gc(g.affine_select(T.eb[:, 512 * b:512 * b + 512], T.ones[:], [[-1, 512]], A.is_equal, 0.0, b, 4))
            need("v", "sg", g3)
            v(V.tensor_scalar(T.hold[:], T.cs[:, 0:C], 2.0, None, A.is_ge))
            v(V.memset(T.irow[:], 0.0))
            v(V.memset(T.prow[:], 0.0))
            vv()
        landed("v", r, "e")
        v(V.tensor_copy(T.einv[:].indirect(e_o[:]), T.iot[:]))
        need("v", "ta", cnt["ta"])
        need("v", "tb", cnt["tb"])
        v(V.tensor_tensor(T.prow[:, 16:336], T.tbt[:].indirect(T.n_o[:]), T.tat[:], A.add))
        vv()
        v(V.transpose(T.tp[:, 0:320], T.prow[:, 16:336]))
        v(V.transpose(T.tp[:, 320:672], T.prow[:, 0:352]))
        landed("v", r, "s")
        v(V.tensor_copy(T.b0[:, 1:C:16], T["sl%d" % r][:]))
        vv()
        v(V.tensor_tensor_scan(T.bf[:], T.hold[:], T.b0[:], 0.0, A.mult, A.add))
        vv()
        n = v(V.transpose(T.sbp[:], T.bf[:]))
        need("s", "sv", n)
        ya = [s(S.activation(rows("yp", k), T.sbp[:], F.Identity, bias=bip[:, k:k + 1], scale=actp[:, k:k + 1])) for k in range(1, 6)]
        vv()
        v(V.tensor_scalar(rows("yp", 0), T.sbp[:], actp[:, 0:1], bip[:, 0:1], A.mult, A.add))
        win = rows("yp", 0)
        for k in range(1, 6):
            need("v", "sa", ya[k - 1])
            vv()
            out = (T.wa if k % 2 else T.wb)[:]
            v(V.tensor_tensor(out, win.indirect(e_o[:]), rows("yp", k), A.min))
            win = out
        need("v", "tm", cnt["tm"])
        vv()
        v(V.tensor_tensor(T.irow[:, 16:336], win.indirect(T.n_o[:]), T.tmt[:], A.is_lt))
        vv()
        v(V.transpose(T.tin[:, 0:320], T.irow[:, 16:336]))
        nir = v(V.transpose(T.tin[:, 320:672], T.irow[:, 0:352]))
        vv()
        v(V.tensor_tensor_scan(T.sc[:], T.tin[:], T.tp[:], 0.0, A.mult, A.max))
        to_offsets(T.sc, 0)
        vv()
        n1 = v(V.tensor_scalar(bi_, po_, 9, 511, A.logical_shift_right, A.bitwise_and))
        n2 = v(V.tensor_scalar(ai_, po_, 511, None, A.bitwise_and))
        vv(n1)
        nb = v(V.tensor_copy(T.b_o[:], bi_))
        vv(n2)
        na = v(V.tensor_copy(T.a_o[:], ai_))
        need("s", "sv", nb)
        za = [[s(S.activation(T.zb[:, C * k + HALF * h:C * k + HALF * h + HALF], T.xh[:, C * k:C * k + C].indirect(T.b_o[:, 10 * h:10 * h + 10]), F.Copy)) for k in range(4)] for h in range(2)]
        tz = []
        if r == 0:
            need("p", "ldw", 32)
        for h in range(2):
            for k in range(4):
                need("v", "sa", za[h][k])
                vv(na)
                v(V.tensor_tensor(T.z[:, 4 * HALF * h + k:4 * HALF * h + 4 * HALF:4], T.xh[:, C * k:C * k + C].indirect(T.a_o[:, 10 * h:10 * h + 10]), T.zb[:, C * k + HALF * h:C * k + HALF * h + HALF], A.add))
            vv()
            lo, hi = HALF * h, HALF * h + HALF
            need("p", "sv", v(V.quantize_mx(T.qz[:, lo:hi], T.pz[:, lo:hi], T.z[:, 4 * lo:4 * hi])))
            tz.append([p(P.matmul_mx(ps[4 * h + b][:, 0:HALF], T.qw[:, 128 * b:128 * b + 128], T.pw[:, 128 * b:128 * b + 128], T.qz[:, lo:hi], T.pz[:, lo:hi], True, True)) for b in range(4)])
        qh, ph = T["qh%d" % r], T["ph%d" % r]
        for b in range(4):
            need("s", "st", tz[0][b])
            ha = s(S.activation(T.h[:, b:4 * HALF:4], ps[b][:, 0:HALF], F.Copy, scale=0.03125))
        for b in range(2):
            need("s", "st", tz[1][b])
            hb = s(S.activation(T.h[:, 4 * HALF + b:4 * C:4], ps[4 + b][:, 0:HALF], F.Copy, scale=0.03125))
        need("v", "sa", ha)
        n1 = v(V.quantize_mx(qh[:, 0:HALF], ph[:, 0:HALF], T.h[:, 0:4 * HALF]))
        for b in range(2, 4):
            need("v", "st", tz[1][b])
            vb = v(V.tensor_scalar(T.h[:, 4 * HALF + b:4 * C:4], ps[4 + b][:, 0:HALF], 0.03125, None, A.mult))
        need("v", "sa", hb)
        vv()
        n2 = v(V.quantize_mx(qh[:, HALF:C], ph[:, HALF:C], T.h[:, 4 * HALF:4 * C]))
        need("g", "sv", n1)
        send(peer(r), T["ql%d" % r][:, 0:HALF].bitcast(dt.uint8), qh[:, 0:HALF].bitcast(dt.uint8), "ca%d" % r)
        need("g", "sv", n2)
        send(peer(r), T["ql%d" % r][:, HALF:FAR].bitcast(dt.uint8), qh[:, HALF:FAR].bitcast(dt.uint8), "cb%d" % r)
        send(peer(r), T["pl%d" % r][:, 0:FAR], ph[:, 0:FAR], "cp%d" % r)
        if r == 0:
            v(V.memset(T.irow2[:], 0.0))
            vv()
            need("s", "sv", cnt["sv"])
        ni = s(S.activation(T.irow2[:, 16:336], T.irow[:, 16:336].indirect(T.n_o[:]), F.Copy))
        for b in range(4):
            if b == 2:
                need("s", "sv", vb)
            s(S.activation(T.j[:, C * b + FAR:C * b + C], ps[4 + b][:, FAR - HALF:HALF], F.Copy, scale=0.03125))
        v(V.tensor_scalar(ki_, po_, 18, None, A.logical_shift_right))
        if r == 0:
            v(V.tensor_scalar(T.mask[:], T.cs[:, 0:C], sl, None, A.is_equal))
            v(V.tensor_scalar(T.seg[:], T.cs[:, 0:C], 1.0, None, A.is_ge))
            v(V.tensor_scalar(T.kt[:], T.cs[:], -1.0, 6.0, A.mult, A.add))
            vv()
            v(V.tensor_tensor(T.xm[:], rows("ar", 0).indirect(T.n_o[:]), T.mask[:], A.mult))
            scan_pick(T.xm[:], T.parf[:])
            vv()
            v(V.tensor_scalar(T.dnf[:], T.parf[:], UNIT, None, A.subtract))
            vv()
            v(V.tensor_tensor(T.ddif[:], T.dnf[:], d_f[:], A.subtract))
        need("v", "sa", ni)
        v(V.transpose(T.tin2[:, 0:320], T.irow2[:, 16:336]))
        v(V.transpose(T.tin2[:, 320:672], T.irow2[:, 0:352]))
        vv()
        v(V.tensor_tensor_scan(T.sc2[:], T.tin2[:], T.kt[:], 0.0, A.mult, A.max))
        to_offsets(T.sc2, 80)
        vv()
        v(V.tensor_tensor(par_, ki_, k2_, A.add))
        vv()
        v(V.tensor_scalar(par_, par_, 1, None, A.bitwise_and))
        vv()
        v(V.tensor_copy(T.parf[:], par_))
        vv()
        v(V.tensor_tensor(T.parf[:], T.parf[:], T.ddif[:], A.mult))
        vv()
        v(V.tensor_tensor(f_f[:], d_f[:], T.parf[:], A.add))
        vv()
        nf = v(V.tensor_copy(f_o[:], f_f[:]))
        if r < 2:
            need("g", "sv", nf)
            send(peer(r + 1), T["el%d" % (r + 1)][:], f_o[:], "e%d" % (r + 1))
        vv()
        v(V.tensor_tensor(T.xm[:], T.einv[:].indirect(f_o[:]), T.mask[:], A.mult))
        nl = scan_pick(T.xm[:], T.l_o[:])
        need("s", "sv", nf)
        if r < 2:
            own_places(f_o, range(1, 5))
            v(V.tensor_scalar(T.dnf[:], T.parf[:], -2.0, None, A.mult))
            vv()
            v(V.tensor_tensor(T.ddif[:], T.ddif[:], T.dnf[:], A.add))
        else:
            n = s(S.activation(rows("ar", 0), T.iot[:].indirect(f_o[:]), F.Copy))
            need("y", "sa", n)
            Y.dma_start(T.dn[:], rows("ar", 0, 0)).then_inc(T.sem.out, 16)
        if r == 0:
            need("v", "sg", g4)
            v(V.quantize_mx(T.qe[:], T.pe[:], T.eb[:]))
            need("p", "sv", cnt["sv"])
        if r == 1:
            need("v", "ldv", 16)
            v(V.quantize_mx(T.qv[:], T.pv[:], T.vt[:]))
        need("p", "sa", ha)
        need("p", "sv", vb)
        for k in ("ca", "cb", "cp"):
            landed("p", r, k)
        for b in range(4):
            td = p(P.matmul_mx(ps[b][:, 0:FAR], T.qe[:, 128 * b:128 * b + 128], T.pe[:, 128 * b:128 * b + 128], T["ql%d" % r][:], T["pl%d" % r][:], True, True))
            need("s", "st", td)
            ja = s(S.activation(T.j[:, C * b:C * b + FAR], ps[b][:, 0:FAR], F.Copy))
            need("v", "sa", ja)
            vv(nl)
            v(V.tensor_tensor(xn[:, b:4 * C:4], T.j[:, C * b:C * b + C].indirect(T.l_o[:]), x[:, b:4 * C:4], A.add))
        if r < 2:
            own_places(f_o, range(5, 7))
            landed("s", r + 1, "e")
            far_places(T["el%d" % (r + 1)], range(1, 3))

    vv()
    n = v(V.quantize_mx(T.qx[:], T.px[:], X[3][:]))
    need("p", "sv", n)
    t = p(P.matmul_mx(ps[0][:, 0:C], T.qv[:], T.pv[:], T.qx[:], T.px[:], True, True))
    need("y", "sv", n)
    need("s", "sv", n)
    Y.dma_start(T.oc[:], T.qx[:].bitcast(dt.uint8)).then_inc(T.sem.out, 16)
    for k in range(4):
        (S if k % 2 else Y).dma_start(T.osc[4 * k:4 * k + 4, :], T.px[32 * k:32 * k + 4, :]).then_inc(T.sem.out, 16)
    need("v", "st", t)
    n = v(V.tensor_copy(T.ts[:], ps[0][:, 0:C]))
    need("y", "sv", n)
    Y.dma_start(T.y[:], T.ts[:]).then_inc(T.sem.out, 16)
    g.wait_ge(T.sem.out, 16 * 7)
    for k in ("sv", "sa", "st", "sg", "sent", "ta", "tb", "tm"):
        need("g", k, cnt[k])
